import numpy as np
import ml_dtypes


def mxq(x, axis, fmt="e4m3"):
    dtype, down = {"e4m3": (ml_dtypes.float8_e4m3fn, 7), "e5m2": (ml_dtypes.float8_e5m2, 14)}[fmt]
    v = np.moveaxis(np.asarray(x, np.float32).astype(ml_dtypes.bfloat16).astype(np.float64), axis, -1)
    blocks = v.reshape(v.shape[:-1] + (-1, 32))
    amax = np.abs(blocks).max(-1, keepdims=True)
    byte = np.maximum(np.where(amax > 0, np.frexp(amax)[1] - 1 + 127, 0) - down, 1)
    scale = np.exp2(byte - 127.0)
    codes = (blocks / scale).astype(np.float32).astype(dtype).astype(np.float64)
    return np.moveaxis((codes * scale).reshape(v.shape), -1, axis)


WIDE = False


def mx_kscale(k):
    if not WIDE:
        return np.ones(k)
    levels = np.array([10, -10, 5, -5, 0])
    if k % 512:
        return np.exp2(np.random.permutation(np.resize(levels, k // 32))).repeat(32)
    a = np.empty((k // 512, 16))
    for p in range(k // 512):
        a[p, :8] = np.random.permutation(np.resize(levels, 8))
        for g in range(8):
            far = levels[np.abs(levels - a[p, g]) >= 10]
            a[p, g + 8] = far[np.random.randint(len(far))]
    return np.exp2(a.ravel()).repeat(32)


BF16 = ml_dtypes.bfloat16


def bf(x):
    return np.asarray(x, np.float32).astype(BF16)


def f64(x):
    return np.asarray(x).astype(np.float64)


E2M1 = np.array([0.0, 0.5, 1.0, 1.5, 2.0, 3.0, 4.0, 6.0, -0.0, -0.5, -1.0, -1.5, -2.0, -3.0, -4.0, -6.0])


def pack_weight(w, fmt):
    k, n = w.shape
    w = f64(bf(w)).reshape(k // 32, 32, n)
    amax = np.abs(w).max(1)
    if fmt == "e4m3":
        byte = np.frexp(amax)[1] - 1 + 127 - 7
    else:
        mant, ex = np.frexp(amax / 6.0)
        byte = np.where(mant > 0.5, ex, ex - 1) + 127
    byte = np.clip(np.where(amax > 0, byte, 1), 1, 254)
    scaled = (w * np.exp2(127.0 - byte)[:, None, :]).reshape(k, n).astype(np.float32)
    by_word = np.ascontiguousarray(scaled.reshape(k // 512, 128, 4, n).transpose(0, 1, 3, 2))
    if fmt == "e4m3":
        words = by_word.astype(ml_dtypes.float8_e4m3fn).view(np.uint8)
    else:
        c = by_word.astype(ml_dtypes.float4_e2m1fn).view(np.uint8) & 0xF
        words = c[..., 0::2] | (c[..., 1::2] << 4)
    return np.ascontiguousarray(words), np.ascontiguousarray(byte.astype(np.uint8).reshape(k // 512, 16, n))


def unpack_weight(words, scales, fmt):
    g, p, n, _ = words.shape
    if fmt == "e4m3":
        vals = np.ascontiguousarray(words).view(ml_dtypes.float8_e4m3fn).astype(np.float64)
    else:
        nib = np.empty((g, p, n, 4), np.uint8)
        nib[..., 0::2] = words & 0xF
        nib[..., 1::2] = words >> 4
        vals = E2M1[nib]
    vals = vals * np.repeat(np.exp2(scales.astype(np.float64) - 127.0), 8, axis=1)[..., None]
    return vals.transpose(0, 1, 3, 2).reshape(g * 512, n)
def pack4(w):
    words, scales = pack_weight(w, "e2m1")
    return words.reshape(words.shape[0], 128, -1), scales


def unpack4(words, scales):
    return unpack_weight(words.reshape(words.shape[0], 128, -1, 2), scales, "e2m1")


def planes(Y):
    n, m = Y.shape
    b = f64(bf(Y)).reshape(n // 32, 32, m)
    amax = np.abs(b).max(1)
    byte = np.clip(np.where(amax > 0, np.frexp(amax)[1] - 1 + 127 - 7, 1), 1, 254)
    codes = (b * np.exp2(127.0 - byte)[:, None, :]).reshape(n, m).astype(np.float32).astype(ml_dtypes.float8_e4m3fn).view(np.uint8)
    words = codes.reshape(n // 512, 128, 4, m).transpose(0, 1, 3, 2)
    return np.ascontiguousarray(words), np.ascontiguousarray(byte.astype(np.uint8).reshape(n // 512, 16, m))


B, I, K, J = 512, 2048, 512, 2048
K2 = 2 * K


def setup_inputs():
    s, t = mx_kscale(I), mx_kscale(K)
    x = bf(np.random.standard_normal((B, I)) * s)
    w_enc_words, w_enc_scales = pack4(np.random.standard_normal((I, K2)) / np.sqrt(I) / s[:, None])
    b_enc = bf(0.3 * np.random.standard_normal(K2))
    eps = bf(np.random.standard_normal((B, K)))
    g = bf((1.0 + 0.1 * np.random.standard_normal(K)) * t)
    w_dec_words, w_dec_scales = pack4(np.random.standard_normal((K, J)) / np.sqrt(K) / t[:, None])
    b_dec = bf(0.5 * np.random.standard_normal(J))
    return {
        "x": x,
        "w_enc_words": w_enc_words,
        "w_enc_scales": w_enc_scales,
        "b_enc": b_enc,
        "eps": eps,
        "g": g,
        "w_dec_words": w_dec_words,
        "w_dec_scales": w_dec_scales,
        "b_dec": b_dec,
    }


def logsumexp_last(l):
    m = np.max(l, axis=-1, keepdims=True)
    return m + np.log(np.sum(np.exp(l - m), axis=-1, keepdims=True))


def core(x, w_enc_words, w_enc_scales, b_enc, eps, g, w_dec_words, w_dec_scales, b_dec):
    w_enc = unpack4(w_enc_words, w_enc_scales)
    w_dec = unpack4(w_dec_words, w_dec_scales)
    k = eps.shape[-1]
    n_items = w_dec.shape[-1]
    h = (mxq(f64(x), 1, "e4m3") @ w_enc) + f64(b_enc)[None, :]
    mu = h[:, :k]
    lv = h[:, k:]
    z = (mu + np.exp(0.5 * lv) * f64(eps)) * f64(g)[None, :]
    l = (mxq(z, 1, "e4m3") @ w_dec) + f64(b_dec)[None, :]
    return l - logsumexp_last(l) + np.log(float(n_items))


def reference(x, w_enc_words, w_enc_scales, b_enc, eps, g, w_dec_words, w_dec_scales, b_dec):
    R_out = core(x, w_enc_words, w_enc_scales, b_enc, eps, g, w_dec_words, w_dec_scales, b_dec)
    words, scales = planes(R_out)
    return R_out, words, scales

@@ -1,0 +1,446 @@
+from contextlib import ExitStack
+
+import concourse.mybir as mybir
+from concourse.masks import make_identity
+
+F32 = mybir.dt.float32
+BF16 = mybir.dt.bfloat16
+I32 = mybir.dt.int32
+U32 = mybir.dt.uint32
+U8 = mybir.dt.uint8
+FP8X4 = mybir.dt.float8_e4m3fn_x4
+FP4X4 = mybir.dt.float4_e2m1fn_x4
+ALU = mybir.AluOpType
+ACT = mybir.ActivationFunctionType
+AX = mybir.AxisListType
+
+P = 128
+B, I, K, J = 512, 2048, 512, 2048
+T = 4
+G1 = I // 512
+FLOPS = 2 * B * I * 2 * K + 2 * B * K * J
+LN2 = 0.6931471805599453
+LNJ = 7.6246189861593985
+
+
+def tile_multvaereparamitemloglift_x2_kernel(
+    tc, x, w_enc_words, w_enc_scales, b_enc, eps, g, w_dec_words, w_dec_scales, b_dec, out_0, out_1, out_2
+):
+    nc = tc.nc
+    with ExitStack() as ctx:
+        keep = ctx.enter_context(tc.tile_pool(name="keep", bufs=1))
+        work = ctx.enter_context(tc.tile_pool(name="work", bufs=2))
+        ph = ctx.enter_context(tc.psum_pool(name="ph", bufs=1))
+        px = ctx.enter_context(tc.psum_pool(name="px", bufs=2))
+        pl = ctx.enter_context(tc.psum_pool(name="pl", bufs=4))
+        ctx.enter_context(tc.manual_schedule())
+
+        x_sb = keep.tile([P, T, I], BF16, name="x_sb", align_bytes=64)
+        we = keep.tile([P, G1, 4 * K], U8, name="we", align_bytes=64)
+        wes = keep.tile([P, G1, 2 * K], U8, name="wes", align_bytes=64)
+        wd = keep.tile([P, 2 * J], U8, name="wd", align_bytes=64)
+        wds = keep.tile([P, J], U8, name="wds", align_bytes=64)
+        eps_sb = keep.tile([P, T, K], BF16, name="eps_sb")
+        brows = keep.tile([P, 512], BF16, name="brows")
+        ident = keep.tile([P, P], F32, name="ident")
+        ident_bf = keep.tile([P, P], BF16, name="ident_bf")
+        consts = keep.tile([P, 3], F32, name="consts")
+        warm = keep.tile([P, 2], F32, name="warm")
+        blv = keep.tile([P, K], F32, name="blv")
+        gb = keep.tile([P, K], BF16, name="gb")
+        bmug = keep.tile([P, K], F32, name="bmug")
+        bdec = keep.tile([P, J], BF16, name="bdec")
+        epsg = keep.tile([P, T, K], F32, name="epsg")
+        l_sb = keep.tile([P, T, J], F32, name="l_sb")
+        o_sb = keep.tile([P, T, J], F32, name="o_sb")
+        pcodes = keep.tile([P, J], U32, name="pcodes", align_bytes=64)
+        pscales = keep.tile([P, J], U8, name="pscales", align_bytes=64)
+
+        x_v = x.rearrange("(p t) k -> p t k", t=T)
+        eps_v = eps.rearrange("(p t) k -> p t k", t=T)
+        out_v = out_0.rearrange("(p t) m -> p t m", t=T)
+
+        wes_w = wes[:].rearrange("p g n -> p (g n)").bitcast(I32)
+        nc.vector.memset(brows[:], 0.0)
+        nc.vector.memset(wes_w[:, 0:512], 0)
+        make_identity(nc, ident[:])
+        nc.gpsimd.memset(wes_w[:, 512:1024], 0)
+        nc.gpsimd.dma_start(out=brows[0:2, :], in_=b_enc.rearrange("(c n) -> c n", c=2))
+        nc.gpsimd.dma_start(out=brows[2:3, :], in_=g.rearrange("(c n) -> c n", c=1))
+        for i in range(3):
+            nc.vector.memset(consts[:, i : i + 1], 1.0 + i)
+        nc.vector.memset(wds[:].bitcast(I32), 0)
+        nc.scalar.activation(warm[:, 1:2], consts[:, 0:1], ACT.Exp)
+
+        nc.sync.dma_start(out=x_sb[:, 0, 0:1024], in_=x_v[:, 0, 0:1024])
+        nc.sync.dma_start(out=x_sb[:, 0, 1024:2048], in_=x_v[:, 0, 1024:2048])
+        nc.sync.dma_start(out=x_sb[:, 1, :], in_=x_v[:, 1, :])
+        for q in range(4):
+            nc.sync.dma_start(
+                out=wes[32 * q : 32 * q + 4].bitcast(I32),
+                in_=w_enc_scales[:, 4 * q : 4 * q + 4, :].rearrange("g q n -> q g n").bitcast(I32),
+            )
+        for k in range(0, G1, 2):
+            nc.sync.dma_start(
+                out=we[:, k : k + 2, :].bitcast(I32),
+                in_=w_enc_words[k : k + 2].rearrange("g p n -> p g n").bitcast(I32),
+            )
+        nc.sync.dma_start(out=eps_sb[:, 0:2, :], in_=eps_v[:, 0:2, :])
+        for q in range(4):
+            nc.sync.dma_start(
+                out=wds[32 * q : 32 * q + 4, :].bitcast(I32),
+                in_=w_dec_scales[0, 4 * q : 4 * q + 4, :].bitcast(I32),
+            )
+        nc.sync.dma_start(out=wd[:].bitcast(I32), in_=w_dec_words[0].bitcast(I32))
+        nc.sync.dma_start(out=x_sb[:, 2, :], in_=x_v[:, 2, :])
+        nc.sync.dma_start(out=bdec[:], in_=b_dec.partition_broadcast(P))
+        nc.sync.dma_start(out=eps_sb[:, 2:4, :], in_=eps_v[:, 2:4, :])
+        nc.sync.dma_start(out=x_sb[:, 3, :], in_=x_v[:, 3, :])
+
+        nc.vector.tensor_copy(out=ident_bf[:], in_=ident[:])
+
+        def x_turn(s, xg, h, eng):
+            xt = px.tile([P, 512], F32, name="xt")
+            words = x_sb[:, s, :].bitcast(F32)
+            for j in range(4):
+                k, u = 2 * h + j // 2, j % 2
+                nc.tensor.transpose(xt[:, 128 * j : 128 * j + 128], words[:, 256 * k + u : 256 * (k + 1) : 2], ident[:])
+            dst = xg[:].bitcast(F32)[:, 512 * h : 512 * h + 512].rearrange("p (k b u) -> p k b u", k=2, u=2)
+            src = xt[:].rearrange("p (k u b) -> p k b u", k=2, u=2)
+            if eng == "s":
+                nc.scalar.copy(out=dst, in_=src)
+            else:
+                nc.vector.tensor_copy(out=dst, in_=src)
+
+        def x_tile():
+            xg = work.tile([P, 4 * 512], BF16, name="xg", align_bytes=64)
+            return xg
+
+        def x_quantize(xg):
+            xc = work.tile([P, 512], U32, name="xc", align_bytes=64)
+            xs = work.tile([P, 512], U8, name="xs", align_bytes=64)
+            nc.vector.quantize_mx(out=xc[:].bitcast(FP8X4), scales=xs[:], in_=xg[:])
+            return xc, xs
+
+        def stage1(xq, early=False):
+            xc, xs = xq
+            if early:
+                lv = pl.tile([P, K], F32, name="l")
+                mu = pl.tile([P, K], F32, name="l")
+            else:
+                lv = ph.tile([P, K], F32, name="h_lv")
+                mu = ph.tile([P, K], F32, name="h_mu")
+            for k in range(G1):
+                for half, acc in ((1, lv), (0, mu)):
+                    nc.tensor.matmul_mx(
+                        out=acc[:],
+                        lhsT=xc[:, 128 * k : 128 * k + 128].bitcast(FP8X4),
+                        lhsT_scale=xs[:, 128 * k : 128 * k + 128],
+                        rhs=we[:, k, 1024 * half : 1024 * half + 1024].bitcast(FP4X4),
+                        rhs_scale=wes[:, k, 512 * half : 512 * half + 512],
+                        start=(k == 0),
+                        stop=(k == G1 - 1),
+                    )
+            return lv, mu
+
+        def lv_bias(lv):
+            a = work.tile([P, K], F32, name="a")
+            nc.vector.tensor_tensor(a[:], lv[:], blv[:], op=ALU.add)
+            return a
+
+        def lv_exp(a):
+            e = work.tile([P, K], F32, name="e")
+            nc.scalar.activation(e[:], a[:], ACT.Exp, scale=0.5)
+            return e
+
+        def mu_gain(mu):
+            t1 = work.tile([P, K], F32, name="t1")
+            nc.vector.tensor_tensor(t1[:], mu[:], gb[:], op=ALU.mult)
+            return t1
+
+        def mu_bias(t1):
+            t2 = work.tile([P, K], F32, name="t2")
+            nc.gpsimd.tensor_tensor(t2[:], t1[:], bmug[:], op=ALU.add)
+            return t2
+
+        def z_gain(s, e, eng):
+            w = work.tile([P, K], F32, name="w")
+            eng.tensor_tensor(w[:], e[:], epsg[:, s, :], op=ALU.mult)
+            return w
+
+        def z_sum(t2, w, eng):
+            z = work.tile([P, K], BF16, name="z")
+            eng.tensor_tensor(z[:], t2[:], w[:], op=ALU.add)
+            return z
+
+        def z_turn(z):
+            zt = px.tile([P, 256], F32, name="xt")
+            words = z[:].bitcast(F32)
+            for u in range(2):
+                nc.tensor.transpose(zt[:, 128 * u : 128 * u + 128], words[:, u:256:2], ident[:])
+            zg = work.tile([P, 512], BF16, name="zg", align_bytes=64)
+            nc.scalar.copy(
+                out=zg[:].bitcast(F32).rearrange("p (b u) -> p b u", u=2),
+                in_=zt[:].rearrange("p (u b) -> p b u", u=2),
+            )
+            return zg
+
+        def z_quantize(zg):
+            zc = work.tile([P, P], U32, name="zc", align_bytes=64)
+            zs = work.tile([P, P], U8, name="zs", align_bytes=64)
+            nc.vector.quantize_mx(out=zc[:].bitcast(FP8X4), scales=zs[:], in_=zg[:])
+            return zc, zs
+
+        def stage2(zq):
+            zc, zs = zq
+            banks = []
+            for c in range(4):
+                acc = pl.tile([P, 512], F32, name="l")
+                nc.tensor.matmul_mx(
+                    out=acc[:],
+                    lhsT=zc[:].bitcast(FP8X4),
+                    lhsT_scale=zs[:],
+                    rhs=wd[:, 1024 * c : 1024 * c + 1024].bitcast(FP4X4),
+                    rhs_scale=wds[:, 512 * c : 512 * c + 512],
+                    start=True,
+                    stop=True,
+                )
+                banks.append(acc)
+            return banks
+
+        def add_bias(s, c, acc):
+            cols = slice(512 * c, 512 * c + 512)
+            nc.vector.tensor_tensor(l_sb[:, s, cols], acc[:], bdec[:, cols], op=ALU.add)
+
+        NEWTON = 4
+
+        def new_stats():
+            st = dict(
+                nm=work.tile([P, 4], F32, name="nm"),
+                part=work.tile([P, 4], F32, name="part"),
+                corr=work.tile([P, 4], F32, name="corr"),
+                prod=work.tile([P, 4], F32, name="prod"),
+                negm=work.tile([P, 1], F32, name="negm"),
+                nmc=work.tile([P, 1], F32, name="nmc"),
+                ssum=work.tile([P, 1], F32, name="ssum"),
+                y=work.tile([P, NEWTON + 1], F32, name="y"),
+                ee=work.tile([P, NEWTON], F32, name="ee"),
+                nco=work.tile([P, 1], F32, name="nco"),
+            )
+            return st
+
+        def part_max(s, st, c):
+            cols = slice(512 * c, 512 * c + 512)
+            nc.vector.tensor_reduce(st["nm"][:, c : c + 1], l_sb[:, s, cols], axis=AX.X, op=ALU.max, negate=True)
+
+        def part_exp(s, st, c):
+            cols = slice(512 * c, 512 * c + 512)
+            junk = work.tile([P, 512], BF16, name="junk")
+            nc.scalar.activation(
+                junk[:], l_sb[:, s, cols], ACT.Exp, bias=st["nm"][:, c : c + 1], accum_out=st["part"][:, c : c + 1]
+            )
+
+        def shift(st):
+            nc.vector.tensor_reduce(st["negm"][:], st["nm"][:], axis=AX.X, op=ALU.min)
+
+        def correct(st):
+            nc.scalar.activation(st["corr"][:], st["nm"][:], ACT.Exp, scale=-1.0, bias=st["negm"][:])
+
+        def merge(st):
+            nc.vector.scalar_tensor_tensor(
+                st["prod"][:], st["corr"][:], 1.0, st["part"][:], op0=ALU.mult, op1=ALU.mult, accum_out=st["ssum"][:]
+            )
+
+        def guess(st):
+            nc.vector.tensor_scalar(
+                st["y"][:, 0:1], st["ssum"][:].bitcast(I32), LN2 * 2.0**-23, -(127.0 - 0.043) * LN2,
+                op0=ALU.mult, op1=ALU.add,
+            )
+
+        def newton_exp(st, i):
+            ee, y = st["ee"], st["y"]
+            if i == 0:
+                nc.scalar.activation(ee[:, 0:1], y[:, 0:1], ACT.Exp, scale=-1.0)
+            else:
+                nc.scalar.activation(ee[:, i : i + 1], y[:, i : i + 1], ACT.Exp, scale=-1.0, bias=consts[:, i - 1 : i])
+
+        def newton_step(st, i, eng):
+            ee, y = st["ee"], st["y"]
+            eng.tensor_scalar(
+                y[:, i + 1 : i + 2], ee[:, i : i + 1], st["ssum"][:], y[:, i : i + 1], op0=ALU.mult, op1=ALU.add
+            )
+
+        def offset0(st, eng):
+            eng.tensor_scalar(st["nmc"][:], st["negm"][:], NEWTON + LNJ, 1.0, op0=ALU.add, op1=ALU.mult)
+
+        def offset1(st, eng):
+            eng.tensor_tensor(st["nco"][:], st["nmc"][:], st["y"][:, NEWTON : NEWTON + 1], op=ALU.subtract)
+
+        def finish(s, st, cols, eng):
+            nco = st["nco"]
+            if eng == "g":
+                nc.gpsimd.tensor_scalar(o_sb[:, s, cols], l_sb[:, s, cols], 1.0, nco[:], op0=ALU.mult, op1=ALU.add)
+            elif eng == "v":
+                nc.vector.tensor_scalar(o_sb[:, s, cols], l_sb[:, s, cols], nco[:], None, op0=ALU.add)
+            else:
+                nc.scalar.activation(o_sb[:, s, cols], l_sb[:, s, cols], ACT.Identity, bias=nco[:])
+
+        def spread(row):
+            acc = pl.tile([P, 512], F32, name="l")
+            nc.tensor.matmul(
+                acc[:], lhsT=ident_bf[:, row : row + 1].to_broadcast([P, P]), rhs=brows[:], start=True, stop=True
+            )
+            return acc
+
+        def eps_gain(s):
+            nc.gpsimd.tensor_tensor(epsg[:, s, :], eps_sb[:, s, :], gb[:], op=ALU.mult)
+
+        V, S, G = nc.vector, nc.scalar, nc.gpsimd
+        xg = x_tile()
+        x_turn(0, xg, 0, "s")
+        x_turn(0, xg, 1, "v")
+        xq0 = x_quantize(xg)
+        xg = x_tile()
+        x_turn(1, xg, 0, "s")
+        x_turn(1, xg, 1, "s")
+        acc = spread(2)
+        nc.vector.tensor_copy(out=gb[:], in_=acc[:])
+        acc = spread(1)
+        nc.scalar.copy(out=blv[:], in_=acc[:])
+        acc = spread(0)
+        nc.vector.tensor_tensor(bmug[:], acc[:], gb[:], op=ALU.mult)
+        xq1 = x_quantize(xg)
+        eps_gain(0)
+        eps_gain(1)
+        lv0, mu0 = stage1(xq0)
+        lv1, mu1 = stage1(xq1, early=True)
+        a = lv_bias(lv0)
+        e0 = lv_exp(a)
+        t1 = mu_gain(mu0)
+        t2 = mu_bias(t1)
+        w0 = z_gain(0, e0, V)
+        a = lv_bias(lv1)
+        e1 = lv_exp(a)
+        z = z_sum(t2, w0, V)
+        xg = x_tile()
+        x_turn(2, xg, 0, "s")
+        zg = z_turn(z)
+        x_turn(2, xg, 1, "s")
+        t1 = mu_gain(mu1)
+        t2 = mu_bias(t1)
+        zq = z_quantize(zg)
+        banks = stage2(zq)
+        xq = x_quantize(xg)
+        lv, mu = stage1(xq)
+        w = z_gain(1, e1, G)
+        z = z_sum(t2, w, G)
+        eps_gain(2)
+        eps_gain(3)
+
+        prev = None
+        for s in range(T):
+            st = new_stats()
+            nxt = s + 1 < T
+            far = s + 2 < T
+            add_bias(s, 0, banks[0])
+            add_bias(s, 1, banks[1])
+            if prev:
+                merge(prev)
+                guess(prev)
+                newton_exp(prev, 0)
+            part_max(s, st, 0)
+            part_exp(s, st, 0)
+            add_bias(s, 2, banks[2])
+            if prev:
+                newton_step(prev, 0, V)
+                newton_exp(prev, 1)
+            part_max(s, st, 1)
+            if nxt:
+                zg = z_turn(z)
+            add_bias(s, 3, banks[3])
+            if prev:
+                newton_step(prev, 1, V)
+                newton_exp(prev, 2)
+            part_exp(s, st, 1)
+            part_max(s, st, 2)
+            if prev:
+                newton_step(prev, 2, V)
+                newton_exp(prev, 3)
+            part_exp(s, st, 2)
+            if nxt:
+                zq = z_quantize(zg)
+                banks = stage2(zq)
+            if far:
+                a = lv_bias(lv)
+                e = lv_exp(a)
+            part_max(s, st, 3)
+            part_exp(s, st, 3)
+            if prev:
+                newton_step(prev, 3, V)
+                offset0(prev, V)
+                offset1(prev, V)
+            shift(st)
+            if far:
+                t1 = mu_gain(mu)
+                t2 = mu_bias(t1)
+            correct(st)
+            if s == 0:
+                xg = x_tile()
+                x_turn(3, xg, 0, "s")
+                x_turn(3, xg, 1, "s")
+            if far:
+                w = z_gain(s + 2, e, G)
+                z = z_sum(t2, w, G)
+            if s == 0:
+                xq = x_quantize(xg)
+                lv, mu = stage1(xq)
+            if prev:
+                finish(s - 1, prev, slice(0, 1024), "g")
+                finish(s - 1, prev, slice(1024, 2048), "g")
+                nc.sync.dma_start(out=out_v[:, s - 1, :], in_=o_sb[:, s - 1, :])
+            prev = st
+
+        s = T - 1
+        pgs = []
+        for c in range(4):
+            pg = keep.tile([P, 512, T], BF16, name="pg" + str(c), align_bytes=64)
+            pgs.append(pg)
+
+        def early_part(h):
+            c, m = h // 2, 256 * (h % 2)
+            nc.vector.tensor_copy(
+                out=pgs[c][:, m : m + 256, 0:3],
+                in_=o_sb[:, 0:3, 512 * c + m : 512 * c + m + 256].rearrange("p t m -> p m t"),
+            )
+
+        for h in range(2):
+            early_part(h)
+        merge(prev)
+        guess(prev)
+        offset0(prev, V)
+        for i in range(NEWTON):
+            newton_exp(prev, i)
+            early_part(2 + i)
+            newton_step(prev, i, V)
+        offset1(prev, V)
+        words_v = out_1[0].rearrange("p m t -> p (m t)")
+        for c in range(4):
+            cols = slice(512 * c, 512 * c + 512)
+            finish(s, prev, cols, "s")
+            nc.sync.dma_start(out=out_v[:, s, cols], in_=o_sb[:, s, cols])
+            if c == 3:
+                early_part(6)
+                early_part(7)
+            nc.vector.tensor_scalar(pgs[c][:, :, 3], l_sb[:, s, cols], prev["nco"][:], None, op0=ALU.add)
+            nc.vector.quantize_mx(
+                out=pcodes[:, cols].bitcast(FP8X4),
+                scales=pscales[:, cols],
+                in_=pgs[c][:].rearrange("p m t -> p (m t)"),
+            )
+            nc.sync.dma_start(
+                out=words_v[:, 2048 * c : 2048 * c + 2048].bitcast(I32), in_=pcodes[:, cols].bitcast(I32)
+            )
+        for q in range(4):
+            nc.sync.dma_start(
+                out=out_2[0, 4 * q : 4 * q + 4, :].bitcast(I32), in_=pscales[32 * q : 32 * q + 4, :].bitcast(I32)
+            )

@@ -44,7 +44,7 @@ def tile_multvaereparamitemloglift_x2_kernel(
         brows = keep.tile([P, 512], BF16, name="brows")
         ident = keep.tile([P, P], F32, name="ident")
         ident_bf = keep.tile([P, P], BF16, name="ident_bf")
-        consts = keep.tile([P, 3], F32, name="consts")
+        consts = keep.tile([P, 4], F32, name="consts")
         warm = keep.tile([P, 2], F32, name="warm")
         blv = keep.tile([P, K], F32, name="blv")
         gb = keep.tile([P, K], BF16, name="gb")
@@ -62,40 +62,43 @@ def tile_multvaereparamitemloglift_x2_kernel(
 
         wes_w = wes[:].rearrange("p g n -> p (g n)").bitcast(I32)
         nc.vector.memset(brows[:], 0.0)
-        nc.vector.memset(wes_w[:, 0:512], 0)
+        nc.vector.memset(wes_w, 0)
         make_identity(nc, ident[:])
-        nc.gpsimd.memset(wes_w[:, 512:1024], 0)
         nc.gpsimd.dma_start(out=brows[0:2, :], in_=b_enc.rearrange("(c n) -> c n", c=2))
         nc.gpsimd.dma_start(out=brows[2:3, :], in_=g.rearrange("(c n) -> c n", c=1))
-        for i in range(3):
-            nc.vector.memset(consts[:, i : i + 1], 1.0 + i)
+        for i in range(4):
+            nc.gpsimd.memset(consts[:, i : i + 1], 1.0 + i)
         nc.vector.memset(wds[:].bitcast(I32), 0)
-        nc.scalar.activation(warm[:, 1:2], consts[:, 0:1], ACT.Exp)
+        nc.vector.memset(warm[:], 0.0)
+        nc.scalar.activation(warm[:, 1:2], warm[:, 0:1], ACT.Exp)
+
+        def load_w(k):
+            nc.sync.dma_start(
+                out=we[:, k : k + 2, :].bitcast(I32),
+                in_=w_enc_words[k : k + 2].rearrange("g p n -> p g n").bitcast(I32),
+            )
 
         nc.sync.dma_start(out=x_sb[:, 0, 0:1024], in_=x_v[:, 0, 0:1024])
         nc.sync.dma_start(out=x_sb[:, 0, 1024:2048], in_=x_v[:, 0, 1024:2048])
-        nc.sync.dma_start(out=x_sb[:, 1, :], in_=x_v[:, 1, :])
         for q in range(4):
             nc.sync.dma_start(
                 out=wes[32 * q : 32 * q + 4].bitcast(I32),
                 in_=w_enc_scales[:, 4 * q : 4 * q + 4, :].rearrange("g q n -> q g n").bitcast(I32),
             )
-        for k in range(0, G1, 2):
-            nc.sync.dma_start(
-                out=we[:, k : k + 2, :].bitcast(I32),
-                in_=w_enc_words[k : k + 2].rearrange("g p n -> p g n").bitcast(I32),
-            )
+        load_w(0)
+        nc.sync.dma_start(out=x_sb[:, 1, :], in_=x_v[:, 1, :])
+        load_w(2)
         nc.sync.dma_start(out=eps_sb[:, 0:2, :], in_=eps_v[:, 0:2, :])
+        nc.sync.dma_start(out=x_sb[:, 2, :], in_=x_v[:, 2, :])
         for q in range(4):
             nc.sync.dma_start(
                 out=wds[32 * q : 32 * q + 4, :].bitcast(I32),
                 in_=w_dec_scales[0, 4 * q : 4 * q + 4, :].bitcast(I32),
             )
         nc.sync.dma_start(out=wd[:].bitcast(I32), in_=w_dec_words[0].bitcast(I32))
-        nc.sync.dma_start(out=x_sb[:, 2, :], in_=x_v[:, 2, :])
         nc.sync.dma_start(out=bdec[:], in_=b_dec.partition_broadcast(P))
-        nc.sync.dma_start(out=eps_sb[:, 2:4, :], in_=eps_v[:, 2:4, :])
         nc.sync.dma_start(out=x_sb[:, 3, :], in_=x_v[:, 3, :])
+        nc.sync.dma_start(out=eps_sb[:, 2:4, :], in_=eps_v[:, 2:4, :])
 
         nc.vector.tensor_copy(out=ident_bf[:], in_=ident[:])
 
@@ -122,18 +125,21 @@ def tile_multvaereparamitemloglift_x2_kernel(
             nc.vector.quantize_mx(out=xc[:].bitcast(FP8X4), scales=xs[:], in_=xg[:])
             return xc, xs
 
-        def stage1(xq, early=False):
-            xc, xs = xq
+        def hidden(early=False):
             if early:
                 lv = pl.tile([P, K], F32, name="l")
                 mu = pl.tile([P, K], F32, name="l")
             else:
                 lv = ph.tile([P, K], F32, name="h_lv")
                 mu = ph.tile([P, K], F32, name="h_mu")
-            for k in range(G1):
-                for half, acc in ((1, lv), (0, mu)):
+            return lv, mu
+
+        def stage1(xq, acc, groups):
+            xc, xs = xq
+            for k in groups:
+                for half in (1, 0):
                     nc.tensor.matmul_mx(
-                        out=acc[:],
+                        out=acc[1 - half][:],
                         lhsT=xc[:, 128 * k : 128 * k + 128].bitcast(FP8X4),
                         lhsT_scale=xs[:, 128 * k : 128 * k + 128],
                         rhs=we[:, k, 1024 * half : 1024 * half + 1024].bitcast(FP4X4),
@@ -141,7 +147,6 @@ def tile_multvaereparamitemloglift_x2_kernel(
                         start=(k == 0),
                         stop=(k == G1 - 1),
                     )
-            return lv, mu
 
         def lv_bias(lv):
             a = work.tile([P, K], F32, name="a")
@@ -214,20 +219,29 @@ def tile_multvaereparamitemloglift_x2_kernel(
 
         NEWTON = 4
 
-        def new_stats():
-            st = dict(
-                nm=work.tile([P, 4], F32, name="nm"),
-                part=work.tile([P, 4], F32, name="part"),
-                corr=work.tile([P, 4], F32, name="corr"),
-                prod=work.tile([P, 4], F32, name="prod"),
-                negm=work.tile([P, 1], F32, name="negm"),
-                nmc=work.tile([P, 1], F32, name="nmc"),
-                ssum=work.tile([P, 1], F32, name="ssum"),
-                y=work.tile([P, NEWTON + 1], F32, name="y"),
-                ee=work.tile([P, NEWTON], F32, name="ee"),
-                nco=work.tile([P, 1], F32, name="nco"),
-            )
+        NEWTON = 4
+
+        def new_stats(s):
+            st = {}
+            for name, n in (("nm", 4), ("part", 4), ("corr", 4), ("prod", 4), ("negm", 1), ("nmc", 1), ("ssum", 1),
+                            ("sj", 1), ("y", NEWTON + 1), ("ee", NEWTON), ("nco", 1)):
+                st[name] = keep.tile([P, n], F32, name=name + str(s))
             return st
+
+        def full_max(s, st):
+            nc.vector.tensor_reduce(st["negm"][:], l_sb[:, s, :], axis=AX.X, op=ALU.max, negate=True)
+
+        def full_exp(s, st):
+            junk = work.tile([P, J], BF16, name="junkf")
+            nc.scalar.activation(junk[:], l_sb[:, s, :], ACT.Exp, bias=st["negm"][:], accum_out=st["ssum"][:])
+
+        def half_max(s, st, h):
+            nc.vector.tensor_reduce(
+                st["nm"][:, h : h + 1], l_sb[:, s, 1024 * h : 1024 * h + 1024], axis=AX.X, op=ALU.max, negate=True
+            )
+
+        def half_shift(st):
+            nc.vector.tensor_tensor(st["negm"][:], st["nm"][:, 0:1], st["nm"][:, 1:2], op=ALU.min)
 
         def part_max(s, st, c):
             cols = slice(512 * c, 512 * c + 512)
@@ -251,11 +265,16 @@ def tile_multvaereparamitemloglift_x2_kernel(
                 st["prod"][:], st["corr"][:], 1.0, st["part"][:], op0=ALU.mult, op1=ALU.mult, accum_out=st["ssum"][:]
             )
 
+        def log_table(st):
+            nc.scalar.activation(st["y"][:, 0:1], st["ssum"][:], ACT.Ln, scale=1.0 / J)
+            nc.scalar.activation(st["nco"][:], st["y"][:, 0:1], ACT.Identity, scale=-1.0, bias=st["negm"][:])
+
         def guess(st):
-            nc.vector.tensor_scalar(
-                st["y"][:, 0:1], st["ssum"][:].bitcast(I32), LN2 * 2.0**-23, -(127.0 - 0.043) * LN2,
-                op0=ALU.mult, op1=ALU.add,
+            nc.scalar.activation(
+                st["y"][:, 0:1], st["ssum"][:].bitcast(U32), ACT.Copy,
+                scale=LN2 * 2.0**-23, bias=-(127.0 - 0.043 + 11.0) * LN2,
             )
+            nc.scalar.activation(st["sj"][:], st["ssum"][:], ACT.Copy, scale=1.0 / J)
 
         def newton_exp(st, i):
             ee, y = st["ee"], st["y"]
@@ -264,17 +283,17 @@ def tile_multvaereparamitemloglift_x2_kernel(
             else:
                 nc.scalar.activation(ee[:, i : i + 1], y[:, i : i + 1], ACT.Exp, scale=-1.0, bias=consts[:, i - 1 : i])
 
-        def newton_step(st, i, eng):
+        def newton_step(st, i):
             ee, y = st["ee"], st["y"]
-            eng.tensor_scalar(
-                y[:, i + 1 : i + 2], ee[:, i : i + 1], st["ssum"][:], y[:, i : i + 1], op0=ALU.mult, op1=ALU.add
+            nc.scalar.activation(
+                y[:, i + 1 : i + 2], ee[:, i : i + 1], ACT.Identity, scale=st["sj"][:], bias=y[:, i : i + 1]
             )
 
-        def offset0(st, eng):
-            eng.tensor_scalar(st["nmc"][:], st["negm"][:], NEWTON + LNJ, 1.0, op0=ALU.add, op1=ALU.mult)
-
-        def offset1(st, eng):
-            eng.tensor_tensor(st["nco"][:], st["nmc"][:], st["y"][:, NEWTON : NEWTON + 1], op=ALU.subtract)
+        def offset(st):
+            nc.scalar.activation(st["nmc"][:], st["negm"][:], ACT.Identity, bias=consts[:, NEWTON - 1 : NEWTON])
+            nc.scalar.activation(
+                st["nco"][:], st["y"][:, NEWTON : NEWTON + 1], ACT.Identity, scale=-1.0, bias=st["nmc"][:]
+            )
 
         def finish(s, st, cols, eng):
             nco = st["nco"]
@@ -296,109 +315,150 @@ def tile_multvaereparamitemloglift_x2_kernel(
             nc.gpsimd.tensor_tensor(epsg[:, s, :], eps_sb[:, s, :], gb[:], op=ALU.mult)
 
         V, S, G = nc.vector, nc.scalar, nc.gpsimd
+        every = range(G1)
         xg = x_tile()
         x_turn(0, xg, 0, "s")
         x_turn(0, xg, 1, "v")
         xq0 = x_quantize(xg)
-        xg = x_tile()
-        x_turn(1, xg, 0, "s")
-        x_turn(1, xg, 1, "s")
         acc = spread(2)
         nc.vector.tensor_copy(out=gb[:], in_=acc[:])
         acc = spread(1)
         nc.scalar.copy(out=blv[:], in_=acc[:])
         acc = spread(0)
         nc.vector.tensor_tensor(bmug[:], acc[:], gb[:], op=ALU.mult)
-        xq1 = x_quantize(xg)
+        xg = x_tile()
+        x_turn(1, xg, 0, "s")
+        x_turn(1, xg, 1, "s")
         eps_gain(0)
         eps_gain(1)
-        lv0, mu0 = stage1(xq0)
-        lv1, mu1 = stage1(xq1, early=True)
-        a = lv_bias(lv0)
+        h0 = hidden()
+        stage1(xq0, h0, every)
+        xq1 = x_quantize(xg)
+        h1 = hidden(early=True)
+        stage1(xq1, h1, every)
+        a = lv_bias(h0[0])
         e0 = lv_exp(a)
-        t1 = mu_gain(mu0)
+        t1 = mu_gain(h0[1])
         t2 = mu_bias(t1)
         w0 = z_gain(0, e0, V)
-        a = lv_bias(lv1)
-        e1 = lv_exp(a)
-        z = z_sum(t2, w0, V)
+        a = lv_bias(h1[0])
         xg = x_tile()
         x_turn(2, xg, 0, "s")
-        zg = z_turn(z)
+        e1 = lv_exp(a)
+        z = z_sum(t2, w0, V)
         x_turn(2, xg, 1, "s")
-        t1 = mu_gain(mu1)
+        zg = z_turn(z)
+        t1 = mu_gain(h1[1])
         t2 = mu_bias(t1)
         zq = z_quantize(zg)
         banks = stage2(zq)
         xq = x_quantize(xg)
-        lv, mu = stage1(xq)
+        h2 = hidden()
+        stage1(xq, h2, every)
         w = z_gain(1, e1, G)
         z = z_sum(t2, w, G)
         eps_gain(2)
-        eps_gain(3)
+        zg = z_turn(z)
+        xg = x_tile()
+        x_turn(3, xg, 0, "s")
+        x_turn(3, xg, 1, "s")
 
-        prev = None
-        for s in range(T):
-            st = new_stats()
-            nxt = s + 1 < T
-            far = s + 2 < T
-            add_bias(s, 0, banks[0])
-            add_bias(s, 1, banks[1])
-            if prev:
-                merge(prev)
-                guess(prev)
-                newton_exp(prev, 0)
-            part_max(s, st, 0)
-            part_exp(s, st, 0)
-            add_bias(s, 2, banks[2])
-            if prev:
-                newton_step(prev, 0, V)
-                newton_exp(prev, 1)
-            part_max(s, st, 1)
-            if nxt:
-                zg = z_turn(z)
-            add_bias(s, 3, banks[3])
-            if prev:
-                newton_step(prev, 1, V)
-                newton_exp(prev, 2)
-            part_exp(s, st, 1)
-            part_max(s, st, 2)
-            if prev:
-                newton_step(prev, 2, V)
-                newton_exp(prev, 3)
-            part_exp(s, st, 2)
-            if nxt:
-                zq = z_quantize(zg)
-                banks = stage2(zq)
-            if far:
-                a = lv_bias(lv)
-                e = lv_exp(a)
-            part_max(s, st, 3)
-            part_exp(s, st, 3)
-            if prev:
-                newton_step(prev, 3, V)
-                offset0(prev, V)
-                offset1(prev, V)
-            shift(st)
-            if far:
-                t1 = mu_gain(mu)
-                t2 = mu_bias(t1)
-            correct(st)
-            if s == 0:
-                xg = x_tile()
-                x_turn(3, xg, 0, "s")
-                x_turn(3, xg, 1, "s")
-            if far:
-                w = z_gain(s + 2, e, G)
-                z = z_sum(t2, w, G)
-            if s == 0:
-                xq = x_quantize(xg)
-                lv, mu = stage1(xq)
-            if prev:
-                finish(s - 1, prev, slice(0, 1024), "g")
-                finish(s - 1, prev, slice(1024, 2048), "g")
-                nc.sync.dma_start(out=out_v[:, s - 1, :], in_=o_sb[:, s - 1, :])
-            prev = st
+        def chain(sts, i):
+            for st in sts:
+                newton_exp(st, i)
+            for st in sts:
+                newton_step(st, i)
+
+        def finished(s, st, engs):
+            for h in range(4):
+                finish(s, st, slice(512 * h, 512 * h + 512), engs[h])
+            nc.sync.dma_start(out=out_v[:, s, :], in_=o_sb[:, s, :])
+
+        sts = [new_stats(s) for s in range(T)]
+        for c in range(4):
+            add_bias(0, c, banks[c])
+        half_max(0, sts[0], 0)
+        a = lv_bias(h2[0])
+        e = lv_exp(a)
+        t1 = mu_gain(h2[1])
+        t2 = mu_bias(t1)
+        w = z_gain(2, e, G)
+        z = z_sum(t2, w, G)
+        zq = z_quantize(zg)
+        banks = stage2(zq)
+        half_max(0, sts[0], 1)
+        half_shift(sts[0])
+        full_exp(0, sts[0])
+        xq = x_quantize(xg)
+        h3 = hidden()
+        stage1(xq, h3, every[0:2])
+        zg = z_turn(z)
+        stage1(xq, h3, every[2:4])
+        eps_gain(3)
+        for c in range(4):
+            add_bias(1, c, banks[c])
+        zq = z_quantize(zg)
+        banks = stage2(zq)
+        a = lv_bias(h3[0])
+        guess(sts[0])
+        chain(sts[0:1], 0)
+        e = lv_exp(a)
+        for i in (1, 2, 3):
+            chain(sts[0:1], i)
+        offset(sts[0])
+        t1 = mu_gain(h3[1])
+        t2 = mu_bias(t1)
+        w = z_gain(3, e, G)
+        z = z_sum(t2, w, G)
+        full_max(1, sts[1])
+        full_exp(1, sts[1])
+        finished(0, sts[0], "gggg")
+        zg = z_turn(z)
+        st = sts[2]
+        for c in range(4):
+            add_bias(2, c, banks[c])
+        part_max(2, st, 0)
+        part_exp(2, st, 0)
+        zq = z_quantize(zg)
+        banks = stage2(zq)
+        for c in (1, 2, 3):
+            part_max(2, st, c)
+        guess(sts[1])
+        chain(sts[1:2], 0)
+        part_exp(2, st, 1)
+        chain(sts[1:2], 1)
+        part_exp(2, st, 2)
+        chain(sts[1:2], 2)
+        part_exp(2, st, 3)
+        shift(st)
+        correct(st)
+        chain(sts[1:2], 3)
+        offset(sts[1])
+        finished(1, sts[1], "gggg")
+        st = sts[3]
+        add_bias(3, 0, banks[0])
+        merge(sts[2])
+        add_bias(3, 1, banks[1])
+        guess(sts[2])
+        part_max(3, st, 0)
+        chain(sts[2:3], 0)
+        part_exp(3, st, 0)
+        add_bias(3, 2, banks[2])
+        chain(sts[2:3], 1)
+        part_max(3, st, 1)
+        part_exp(3, st, 1)
+        chain(sts[2:3], 2)
+        add_bias(3, 3, banks[3])
+        part_max(3, st, 2)
+        chain(sts[2:3], 3)
+        offset(sts[2])
+        part_exp(3, st, 2)
+        part_max(3, st, 3)
+        part_exp(3, st, 3)
+        shift(st)
+        correct(st)
+        finished(2, sts[2], "vvgg")
+        prev = st
 
         s = T - 1
         pgs = []
@@ -413,25 +473,14 @@ def tile_multvaereparamitemloglift_x2_kernel(
                 in_=o_sb[:, 0:3, 512 * c + m : 512 * c + m + 256].rearrange("p t m -> p m t"),
             )
 
-        for h in range(2):
-            early_part(h)
-        merge(prev)
-        guess(prev)
-        offset0(prev, V)
-        for i in range(NEWTON):
-            newton_exp(prev, i)
-            early_part(2 + i)
-            newton_step(prev, i, V)
-        offset1(prev, V)
-        words_v = out_1[0].rearrange("p m t -> p (m t)")
-        for c in range(4):
+        def late_part(c):
             cols = slice(512 * c, 512 * c + 512)
-            finish(s, prev, cols, "s")
-            nc.sync.dma_start(out=out_v[:, s, cols], in_=o_sb[:, s, cols])
-            if c == 3:
-                early_part(6)
-                early_part(7)
             nc.vector.tensor_scalar(pgs[c][:, :, 3], l_sb[:, s, cols], prev["nco"][:], None, op0=ALU.add)
+
+        words_v = out_1[0].rearrange("p m t -> p (m t)")
+
+        def planes(c):
+            cols = slice(512 * c, 512 * c + 512)
             nc.vector.quantize_mx(
                 out=pcodes[:, cols].bitcast(FP8X4),
                 scales=pscales[:, cols],
@@ -440,6 +489,20 @@ def tile_multvaereparamitemloglift_x2_kernel(
             nc.sync.dma_start(
                 out=words_v[:, 2048 * c : 2048 * c + 2048].bitcast(I32), in_=pcodes[:, cols].bitcast(I32)
             )
+
+        early_part(0)
+        merge(prev)
+        log_table(prev)
+        for h in range(1, 8):
+            early_part(h)
+        for c in range(4):
+            cols = slice(512 * c, 512 * c + 512)
+            finish(s, prev, cols, "s")
+            nc.sync.dma_start(out=out_v[:, s, cols], in_=o_sb[:, s, cols])
+            late_part(c)
+            if c > 0:
+                planes(c - 1)
+        planes(3)
         for q in range(4):
             nc.sync.dma_start(
                 out=out_2[0, 4 * q : 4 * q + 4, :].bitcast(I32), in_=pscales[32 * q : 32 * q + 4, :].bitcast(I32)

@@ -42,6 +42,7 @@ def tile_multvaereparamitemloglift_x2_kernel(
         wds = keep.tile([P, J], U8, name="wds", align_bytes=64)
         eps_sb = keep.tile([P, T, K], BF16, name="eps_sb")
         brows = keep.tile([P, 512], BF16, name="brows")
+        zeros = keep.tile([P, 512], BF16, name="zeros")
         ident = keep.tile([P, P], F32, name="ident")
         ident_bf = keep.tile([P, P], BF16, name="ident_bf")
         consts = keep.tile([P, 4], F32, name="consts")
@@ -61,11 +62,13 @@ def tile_multvaereparamitemloglift_x2_kernel(
         out_v = out_0.rearrange("(p t) m -> p t m", t=T)
 
         wes_w = wes[:].rearrange("p g n -> p (g n)").bitcast(I32)
+        nc.vector.memset(zeros[:], 0.0)
         nc.vector.memset(brows[:], 0.0)
         nc.vector.memset(wes_w, 0)
         make_identity(nc, ident[:])
         nc.gpsimd.dma_start(out=brows[0:2, :], in_=b_enc.rearrange("(c n) -> c n", c=2))
         nc.gpsimd.dma_start(out=brows[2:3, :], in_=g.rearrange("(c n) -> c n", c=1))
+        nc.gpsimd.dma_start(out=brows[3:7, :], in_=b_dec.rearrange("(c n) -> c n", c=4))
         for i in range(4):
             nc.gpsimd.memset(consts[:, i : i + 1], 1.0 + i)
         nc.vector.memset(wds[:].bitcast(I32), 0)
@@ -96,14 +99,16 @@ def tile_multvaereparamitemloglift_x2_kernel(
                 in_=w_dec_scales[0, 4 * q : 4 * q + 4, :].bitcast(I32),
             )
         nc.sync.dma_start(out=wd[:].bitcast(I32), in_=w_dec_words[0].bitcast(I32))
-        nc.sync.dma_start(out=bdec[:], in_=b_dec.partition_broadcast(P))
         nc.sync.dma_start(out=x_sb[:, 3, :], in_=x_v[:, 3, :])
         nc.sync.dma_start(out=eps_sb[:, 2:4, :], in_=eps_v[:, 2:4, :])
 
         nc.vector.tensor_copy(out=ident_bf[:], in_=ident[:])
 
-        def x_turn(s, xg, h, eng):
-            xt = px.tile([P, 512], F32, name="xt")
+        def x_turn(s, xg, h, eng, early=False):
+            if early:
+                xt = pl.tile([P, 512], F32, name="l")
+            else:
+                xt = px.tile([P, 512], F32, name="xt")
             words = x_sb[:, s, :].bitcast(F32)
             for j in range(4):
                 k, u = 2 * h + j // 2, j % 2
@@ -163,9 +168,9 @@ def tile_multvaereparamitemloglift_x2_kernel(
             nc.vector.tensor_tensor(t1[:], mu[:], gb[:], op=ALU.mult)
             return t1
 
-        def mu_bias(t1):
+        def mu_bias(t1, eng):
             t2 = work.tile([P, K], F32, name="t2")
-            nc.gpsimd.tensor_tensor(t2[:], t1[:], bmug[:], op=ALU.add)
+            eng.tensor_tensor(t2[:], t1[:], bmug[:], op=ALU.add)
             return t2
 
         def z_gain(s, e, eng):
@@ -254,15 +259,23 @@ def tile_multvaereparamitemloglift_x2_kernel(
                 junk[:], l_sb[:, s, cols], ACT.Exp, bias=st["nm"][:, c : c + 1], accum_out=st["part"][:, c : c + 1]
             )
 
-        def shift(st):
-            nc.vector.tensor_reduce(st["negm"][:], st["nm"][:], axis=AX.X, op=ALU.min)
+        def shift(st, n):
+            nc.vector.tensor_reduce(st["negm"][:], st["nm"][:, 0:n], axis=AX.X, op=ALU.min)
 
-        def correct(st):
-            nc.scalar.activation(st["corr"][:], st["nm"][:], ACT.Exp, scale=-1.0, bias=st["negm"][:])
+        def correct(st, n):
+            nc.scalar.activation(st["corr"][:, 0:n], st["nm"][:, 0:n], ACT.Exp, scale=-1.0, bias=st["negm"][:])
 
-        def merge(st):
+        def merge(st, n):
             nc.vector.scalar_tensor_tensor(
-                st["prod"][:], st["corr"][:], 1.0, st["part"][:], op0=ALU.mult, op1=ALU.mult, accum_out=st["ssum"][:]
+                st["prod"][:, 0:n], st["corr"][:, 0:n], 1.0, st["part"][:, 0:n], op0=ALU.mult, op1=ALU.mult,
+                accum_out=st["ssum"][:],
+            )
+
+        def half_exp(s, st, h):
+            cols = slice(1024 * h, 1024 * h + 1024)
+            junk = work.tile([P, 1024], BF16, name="junkh")
+            nc.scalar.activation(
+                junk[:], l_sb[:, s, cols], ACT.Exp, bias=st["nm"][:, h : h + 1], accum_out=st["part"][:, h : h + 1]
             )
 
         def log_table(st):
@@ -304,6 +317,10 @@ def tile_multvaereparamitemloglift_x2_kernel(
             else:
                 nc.scalar.activation(o_sb[:, s, cols], l_sb[:, s, cols], ACT.Identity, bias=nco[:])
 
+        def warm_up():
+            acc = px.tile([P, 512], F32, name="xt")
+            nc.tensor.matmul(acc[:], lhsT=zeros[:, 0:P], rhs=zeros[:], start=True, stop=True)
+
         def spread(row):
             acc = pl.tile([P, 512], F32, name="l")
             nc.tensor.matmul(
@@ -311,57 +328,75 @@ def tile_multvaereparamitemloglift_x2_kernel(
             )
             return acc
 
-        def eps_gain(s):
-            nc.gpsimd.tensor_tensor(epsg[:, s, :], eps_sb[:, s, :], gb[:], op=ALU.mult)
+        def eps_gain(s, eng):
+            eng.tensor_tensor(epsg[:, s, :], eps_sb[:, s, :], gb[:], op=ALU.mult)
 
         V, S, G = nc.vector, nc.scalar, nc.gpsimd
         every = range(G1)
+        for i in range(4):
+            warm_up()
         xg = x_tile()
         x_turn(0, xg, 0, "s")
         x_turn(0, xg, 1, "v")
         xq0 = x_quantize(xg)
-        acc = spread(2)
-        nc.vector.tensor_copy(out=gb[:], in_=acc[:])
+
+        def dec_row(c, eng):
+            acc = spread(3 + c)
+            cols = slice(512 * c, 512 * c + 512)
+            if eng == "s":
+                nc.scalar.copy(out=bdec[:, cols], in_=acc[:])
+            else:
+                nc.vector.tensor_copy(out=bdec[:, cols], in_=acc[:])
+
         acc = spread(1)
         nc.scalar.copy(out=blv[:], in_=acc[:])
+        acc = spread(2)
+        nc.vector.tensor_copy(out=gb[:], in_=acc[:])
         acc = spread(0)
         nc.vector.tensor_tensor(bmug[:], acc[:], gb[:], op=ALU.mult)
-        xg = x_tile()
-        x_turn(1, xg, 0, "s")
-        x_turn(1, xg, 1, "s")
-        eps_gain(0)
-        eps_gain(1)
+        dec_row(0, "s")
+        dec_row(1, "s")
+        eps_gain(0, G)
         h0 = hidden()
         stage1(xq0, h0, every)
-        xq1 = x_quantize(xg)
-        h1 = hidden(early=True)
-        stage1(xq1, h1, every)
         a = lv_bias(h0[0])
         e0 = lv_exp(a)
         t1 = mu_gain(h0[1])
-        t2 = mu_bias(t1)
+        xg1 = x_tile()
+        x_turn(1, xg1, 0, "s")
+        x_turn(1, xg1, 1, "v")
+        dec_row(2, "s")
+        dec_row(3, "s")
+        t2 = mu_bias(t1, V)
+        eps_gain(1, G)
+        xg2 = x_tile()
+        x_turn(2, xg2, 0, "s")
+        x_turn(2, xg2, 1, "s")
+        xq1 = x_quantize(xg1)
+        h1 = hidden(early=True)
+        stage1(xq1, h1, every[0:2])
         w0 = z_gain(0, e0, V)
-        a = lv_bias(h1[0])
-        xg = x_tile()
-        x_turn(2, xg, 0, "s")
-        e1 = lv_exp(a)
         z = z_sum(t2, w0, V)
-        x_turn(2, xg, 1, "s")
         zg = z_turn(z)
-        t1 = mu_gain(h1[1])
-        t2 = mu_bias(t1)
+        stage1(xq1, h1, every[2:4])
+        xq = x_quantize(xg2)
         zq = z_quantize(zg)
         banks = stage2(zq)
-        xq = x_quantize(xg)
+        a = lv_bias(h1[0])
+        e1 = lv_exp(a)
+        t1 = mu_gain(h1[1])
+        t2 = mu_bias(t1, G)
         h2 = hidden()
         stage1(xq, h2, every)
         w = z_gain(1, e1, G)
         z = z_sum(t2, w, G)
-        eps_gain(2)
+        eps_gain(2, G)
+        xg3 = x_tile()
+        x_turn(3, xg3, 0, "s")
+        x_turn(3, xg3, 1, "s")
         zg = z_turn(z)
-        xg = x_tile()
-        x_turn(3, xg, 0, "s")
-        x_turn(3, xg, 1, "s")
+        warm_up()
+        warm_up()
 
         def chain(sts, i):
             for st in sts:
@@ -372,7 +407,9 @@ def tile_multvaereparamitemloglift_x2_kernel(
         def finished(s, st, engs):
             for h in range(4):
                 finish(s, st, slice(512 * h, 512 * h + 512), engs[h])
-            nc.sync.dma_start(out=out_v[:, s, :], in_=o_sb[:, s, :])
+                if h % 2:
+                    cols = slice(512 * h - 512, 512 * h + 512)
+                    nc.sync.dma_start(out=out_v[:, s, cols], in_=o_sb[:, s, cols])
 
         sts = [new_stats(s) for s in range(T)]
         for c in range(4):
@@ -381,83 +418,76 @@ def tile_multvaereparamitemloglift_x2_kernel(
         a = lv_bias(h2[0])
         e = lv_exp(a)
         t1 = mu_gain(h2[1])
-        t2 = mu_bias(t1)
-        w = z_gain(2, e, G)
-        z = z_sum(t2, w, G)
-        zq = z_quantize(zg)
-        banks = stage2(zq)
+        t2 = mu_bias(t1, G)
         half_max(0, sts[0], 1)
         half_shift(sts[0])
+        zq = z_quantize(zg)
+        xq = x_quantize(xg3)
+        banks = stage2(zq)
         full_exp(0, sts[0])
-        xq = x_quantize(xg)
+        w = z_gain(2, e, G)
+        z = z_sum(t2, w, G)
+        eps_gain(3, G)
         h3 = hidden()
-        stage1(xq, h3, every[0:2])
+        stage1(xq, h3, every)
         zg = z_turn(z)
-        stage1(xq, h3, every[2:4])
-        eps_gain(3)
         for c in range(4):
             add_bias(1, c, banks[c])
+        a = lv_bias(h3[0])
+        e = lv_exp(a)
+        t1 = mu_gain(h3[1])
+        t2 = mu_bias(t1, G)
         zq = z_quantize(zg)
         banks = stage2(zq)
-        a = lv_bias(h3[0])
-        guess(sts[0])
-        chain(sts[0:1], 0)
-        e = lv_exp(a)
-        for i in (1, 2, 3):
-            chain(sts[0:1], i)
-        offset(sts[0])
-        t1 = mu_gain(h3[1])
-        t2 = mu_bias(t1)
         w = z_gain(3, e, G)
         z = z_sum(t2, w, G)
+        guess(sts[0])
+        for i in range(NEWTON):
+            chain(sts[0:1], i)
+        offset(sts[0])
         full_max(1, sts[1])
         full_exp(1, sts[1])
-        finished(0, sts[0], "gggg")
         zg = z_turn(z)
+        finished(0, sts[0], "gggg")
         st = sts[2]
         for c in range(4):
             add_bias(2, c, banks[c])
-        part_max(2, st, 0)
-        part_exp(2, st, 0)
+        half_max(2, st, 0)
         zq = z_quantize(zg)
         banks = stage2(zq)
-        for c in (1, 2, 3):
-            part_max(2, st, c)
         guess(sts[1])
         chain(sts[1:2], 0)
-        part_exp(2, st, 1)
-        chain(sts[1:2], 1)
-        part_exp(2, st, 2)
-        chain(sts[1:2], 2)
-        part_exp(2, st, 3)
-        shift(st)
-        correct(st)
-        chain(sts[1:2], 3)
+        half_exp(2, st, 0)
+        half_max(2, st, 1)
+        for i in (1, 2, 3):
+            chain(sts[1:2], i)
         offset(sts[1])
+        half_exp(2, st, 1)
+        shift(st, 2)
+        correct(st, 2)
         finished(1, sts[1], "gggg")
         st = sts[3]
         add_bias(3, 0, banks[0])
-        merge(sts[2])
         add_bias(3, 1, banks[1])
-        guess(sts[2])
         part_max(3, st, 0)
-        chain(sts[2:3], 0)
-        part_exp(3, st, 0)
         add_bias(3, 2, banks[2])
-        chain(sts[2:3], 1)
+        merge(sts[2], 2)
         part_max(3, st, 1)
-        part_exp(3, st, 1)
-        chain(sts[2:3], 2)
         add_bias(3, 3, banks[3])
         part_max(3, st, 2)
+        part_max(3, st, 3)
+        part_exp(3, st, 0)
+        guess(sts[2])
+        chain(sts[2:3], 0)
+        part_exp(3, st, 1)
+        chain(sts[2:3], 1)
+        part_exp(3, st, 2)
+        chain(sts[2:3], 2)
+        part_exp(3, st, 3)
+        shift(st, 4)
+        correct(st, 4)
         chain(sts[2:3], 3)
         offset(sts[2])
-        part_exp(3, st, 2)
-        part_max(3, st, 3)
-        part_exp(3, st, 3)
-        shift(st)
-        correct(st)
-        finished(2, sts[2], "vvgg")
         prev = st
 
         s = T - 1
@@ -469,13 +499,17 @@ def tile_multvaereparamitemloglift_x2_kernel(
         def early_part(h):
             c, m = h // 2, 256 * (h % 2)
             nc.vector.tensor_copy(
-                out=pgs[c][:, m : m + 256, 0:3],
-                in_=o_sb[:, 0:3, 512 * c + m : 512 * c + m + 256].rearrange("p t m -> p m t"),
+                out=pgs[c][:, m : m + 256, 0:2],
+                in_=o_sb[:, 0:2, 512 * c + m : 512 * c + m + 256].rearrange("p t m -> p m t"),
             )
 
         def late_part(c):
             cols = slice(512 * c, 512 * c + 512)
-            nc.vector.tensor_scalar(pgs[c][:, :, 3], l_sb[:, s, cols], prev["nco"][:], None, op0=ALU.add)
+            src = o_sb[:, 2:4, cols].rearrange("p t m -> p m t")
+            if c > 1:
+                nc.scalar.copy(out=pgs[c][:, :, 2:4], in_=src)
+            else:
+                nc.vector.tensor_copy(out=pgs[c][:, :, 2:4], in_=src)
 
         words_v = out_1[0].rearrange("p m t -> p (m t)")
 
@@ -490,19 +524,23 @@ def tile_multvaereparamitemloglift_x2_kernel(
                 out=words_v[:, 2048 * c : 2048 * c + 2048].bitcast(I32), in_=pcodes[:, cols].bitcast(I32)
             )
 
-        early_part(0)
-        merge(prev)
-        log_table(prev)
-        for h in range(1, 8):
+        for h in range(3):
             early_part(h)
-        for c in range(4):
+        merge(prev, 4)
+        log_table(prev)
+        for h in range(3, 5):
+            early_part(h)
+        finished(2, sts[2], "vvvv")
+        for h in range(5, 8):
+            early_part(h)
+        for c in (0, 1, 3, 2):
             cols = slice(512 * c, 512 * c + 512)
-            finish(s, prev, cols, "s")
+            finish(s, prev, cols, "vsss"[c])
             nc.sync.dma_start(out=out_v[:, s, cols], in_=o_sb[:, s, cols])
+        for c in (0, 1, 3, 2):
             late_part(c)
-            if c > 0:
-                planes(c - 1)
-        planes(3)
+        for c in (0, 1, 3, 2):
+            planes(c)
         for q in range(4):
             nc.sync.dma_start(
                 out=out_2[0, 4 * q : 4 * q + 4, :].bitcast(I32), in_=pscales[32 * q : 32 * q + 4, :].bitcast(I32)

@@ -18,6 +18,7 @@ P = 128
 B, I, K, J = 512, 2048, 512, 2048
 T = 4
 G1 = I // 512
+NEWTON = 4
 FLOPS = 2 * B * I * 2 * K + 2 * B * K * J
 LN2 = 0.6931471805599453
 LNJ = 7.6246189861593985
@@ -27,521 +28,555 @@ def tile_multvaereparamitemloglift_x2_kernel(
     tc, x, w_enc_words, w_enc_scales, b_enc, eps, g, w_dec_words, w_dec_scales, b_dec, out_0, out_1, out_2
 ):
     nc = tc.nc
+    V, S, G = nc.vector, nc.scalar, nc.gpsimd
     with ExitStack() as ctx:
         keep = ctx.enter_context(tc.tile_pool(name="keep", bufs=1))
-        work = ctx.enter_context(tc.tile_pool(name="work", bufs=2))
-        ph = ctx.enter_context(tc.psum_pool(name="ph", bufs=1))
-        px = ctx.enter_context(tc.psum_pool(name="px", bufs=2))
-        pl = ctx.enter_context(tc.psum_pool(name="pl", bufs=4))
+        banks = ctx.enter_context(tc.psum_pool(name="banks", bufs=1))
         ctx.enter_context(tc.manual_schedule())
 
-        x_sb = keep.tile([P, T, I], BF16, name="x_sb", align_bytes=64)
-        we = keep.tile([P, G1, 4 * K], U8, name="we", align_bytes=64)
-        wes = keep.tile([P, G1, 2 * K], U8, name="wes", align_bytes=64)
-        wd = keep.tile([P, 2 * J], U8, name="wd", align_bytes=64)
-        wds = keep.tile([P, J], U8, name="wds", align_bytes=64)
-        eps_sb = keep.tile([P, T, K], BF16, name="eps_sb")
-        brows = keep.tile([P, 512], BF16, name="brows")
-        zeros = keep.tile([P, 512], BF16, name="zeros")
-        ident = keep.tile([P, P], F32, name="ident")
-        ident_bf = keep.tile([P, P], BF16, name="ident_bf")
-        consts = keep.tile([P, 4], F32, name="consts")
-        warm = keep.tile([P, 2], F32, name="warm")
-        blv = keep.tile([P, K], F32, name="blv")
-        gb = keep.tile([P, K], BF16, name="gb")
-        bmug = keep.tile([P, K], F32, name="bmug")
-        bdec = keep.tile([P, J], BF16, name="bdec")
-        epsg = keep.tile([P, T, K], F32, name="epsg")
-        l_sb = keep.tile([P, T, J], F32, name="l_sb")
-        o_sb = keep.tile([P, T, J], F32, name="o_sb")
-        pcodes = keep.tile([P, J], U32, name="pcodes", align_bytes=64)
-        pscales = keep.tile([P, J], U8, name="pscales", align_bytes=64)
+        def sb(name, shape, dtype, align=64):
+            return keep.tile(shape, dtype, name=name, align_bytes=align)
+
+        x_sb = sb("x_sb", [P, T, I], BF16)
+        we = [sb("we" + str(i), [P, G1, 2 * K], U8) for i in range(2)]
+        wes = sb("wes", [P, G1, 2 * K], U8)
+        wd = sb("wd", [P, 2 * J], U8)
+        wds = sb("wds", [P, J], U8)
+        eps_sb = sb("eps_sb", [P, T, K], BF16)
+        zeros = sb("zeros", [P, 512], BF16)
+        rows_h = sb("rows_h", [P, 512], BF16)
+        rows_g = sb("rows_g", [P, 512], BF16)
+        rows_d = sb("rows_d", [P, 512], BF16)
+        ident = sb("ident", [P, P], F32)
+        ident_bf = sb("ident_bf", [P, P], BF16)
+        consts = sb("consts", [P, NEWTON], F32)
+        warm = sb("warm", [P, 2], F32)
+        blv = sb("blv", [P, K], F32)
+        gb = sb("gb", [P, K], BF16)
+        bmu = sb("bmu", [P, K], BF16)
+        bmug = sb("bmug", [P, K], F32)
+        bdec = sb("bdec", [P, J], BF16)
+        epsg = sb("epsg", [P, T, K], F32)
+        l_sb = sb("l_sb", [P, T, J], F32)
+        pcodes = sb("pcodes", [P, J], U32)
+        pscales = sb("pscales", [P, J], U8)
+        pg = sb("pg", [P, J, T], BF16)
+        xg = [sb("xg" + str(s), [P, 2048], BF16) for s in range(3)]
+        xg.append(xg[0])
+        xc = [sb("xc" + str(s), [P, 512], U32) for s in range(T)]
+        xs = [sb("xs" + str(s), [P, 512], U8) for s in range(T)]
+        a = [sb("a" + str(s), [P, K], F32) for s in range(T)]
+        e = [sb("e" + str(s), [P, K], F32) for s in range(T)]
+        t1 = [sb("t1" + str(s), [P, K], F32) for s in range(T)]
+        t2 = [sb("t2" + str(s), [P, K], F32) for s in range(T)]
+        w = [sb("w" + str(s), [P, K], F32) for s in range(T)]
+        z = [sb("z" + str(s), [P, K], BF16) for s in range(T)]
+        zg = [sb("zg" + str(s), [P, 512], BF16) for s in range(T)]
+        zc = [sb("zc" + str(s), [P, P], U32) for s in range(T)]
+        zs = [sb("zs" + str(s), [P, P], U8) for s in range(T)]
+        junk = [sb("junk" + str(s), [P, J], BF16) for s in range(2)]
+        stat = {}
+        for s in range(T):
+            for name, n in (("nm", 4), ("part", 4), ("corr", 4), ("prod", 4), ("negm", 1), ("nmc", 1), ("ssum", 1),
+                            ("sj", 1), ("y", NEWTON + 1), ("ee", NEWTON), ("nco", 1)):
+                stat[name, s] = sb(name + str(s), [P, n], F32, 32)
+        bx = [banks.tile([P, 512], F32, name="bx" + str(i)) for i in range(2)]
+        bh = [banks.tile([P, 512], F32, name="bh" + str(i)) for i in range(2)]
+        bl = [banks.tile([P, 512], F32, name="bl" + str(i)) for i in range(4)]
 
         x_v = x.rearrange("(p t) k -> p t k", t=T)
         eps_v = eps.rearrange("(p t) k -> p t k", t=T)
         out_v = out_0.rearrange("(p t) m -> p t m", t=T)
-
+        words_v = out_1[0].rearrange("p m t -> p (m t)")
         wes_w = wes[:].rearrange("p g n -> p (g n)").bitcast(I32)
-        nc.vector.memset(zeros[:], 0.0)
-        nc.vector.memset(brows[:], 0.0)
-        nc.vector.memset(wes_w, 0)
-        make_identity(nc, ident[:])
-        nc.gpsimd.dma_start(out=brows[0:2, :], in_=b_enc.rearrange("(c n) -> c n", c=2))
-        nc.gpsimd.dma_start(out=brows[2:3, :], in_=g.rearrange("(c n) -> c n", c=1))
-        nc.gpsimd.dma_start(out=brows[3:7, :], in_=b_dec.rearrange("(c n) -> c n", c=4))
-        for i in range(4):
-            nc.gpsimd.memset(consts[:, i : i + 1], 1.0 + i)
-        nc.vector.memset(wds[:].bitcast(I32), 0)
-        nc.vector.memset(warm[:], 0.0)
-        nc.scalar.activation(warm[:, 1:2], warm[:, 0:1], ACT.Exp)
 
-        def load_w(k):
+        def load_w(half):
+            cols = slice(1024 * half, 1024 * half + 1024)
             nc.sync.dma_start(
-                out=we[:, k : k + 2, :].bitcast(I32),
-                in_=w_enc_words[k : k + 2].rearrange("g p n -> p g n").bitcast(I32),
+                out=we[half][:].bitcast(I32), in_=w_enc_words[:, :, cols].rearrange("g p n -> p g n").bitcast(I32)
             )
 
-        nc.sync.dma_start(out=x_sb[:, 0, 0:1024], in_=x_v[:, 0, 0:1024])
-        nc.sync.dma_start(out=x_sb[:, 0, 1024:2048], in_=x_v[:, 0, 1024:2048])
-        for q in range(4):
+        def load_wes(q):
             nc.sync.dma_start(
                 out=wes[32 * q : 32 * q + 4].bitcast(I32),
                 in_=w_enc_scales[:, 4 * q : 4 * q + 4, :].rearrange("g q n -> q g n").bitcast(I32),
             )
-        load_w(0)
-        nc.sync.dma_start(out=x_sb[:, 1, :], in_=x_v[:, 1, :])
-        load_w(2)
-        nc.sync.dma_start(out=eps_sb[:, 0:2, :], in_=eps_v[:, 0:2, :])
-        nc.sync.dma_start(out=x_sb[:, 2, :], in_=x_v[:, 2, :])
-        for q in range(4):
+
+        def load_wds(q):
             nc.sync.dma_start(
-                out=wds[32 * q : 32 * q + 4, :].bitcast(I32),
-                in_=w_dec_scales[0, 4 * q : 4 * q + 4, :].bitcast(I32),
+                out=wds[32 * q : 32 * q + 4, :].bitcast(I32), in_=w_dec_scales[0, 4 * q : 4 * q + 4, :].bitcast(I32)
             )
-        nc.sync.dma_start(out=wd[:].bitcast(I32), in_=w_dec_words[0].bitcast(I32))
-        nc.sync.dma_start(out=x_sb[:, 3, :], in_=x_v[:, 3, :])
-        nc.sync.dma_start(out=eps_sb[:, 2:4, :], in_=eps_v[:, 2:4, :])
 
-        nc.vector.tensor_copy(out=ident_bf[:], in_=ident[:])
+        def warm_up(bank):
+            nc.tensor.matmul(bank[:], lhsT=zeros[:, 0:P], rhs=zeros[:], start=True, stop=True)
 
-        def x_turn(s, xg, h, eng, early=False):
-            if early:
-                xt = pl.tile([P, 512], F32, name="l")
-            else:
-                xt = px.tile([P, 512], F32, name="xt")
+        def spread(rows, row, bank):
+            nc.tensor.matmul(
+                bank[:], lhsT=ident_bf[:, row : row + 1].to_broadcast([P, P]), rhs=rows[:], start=True, stop=True
+            )
+
+        def turn_x(s, h, bank):
             words = x_sb[:, s, :].bitcast(F32)
             for j in range(4):
                 k, u = 2 * h + j // 2, j % 2
-                nc.tensor.transpose(xt[:, 128 * j : 128 * j + 128], words[:, 256 * k + u : 256 * (k + 1) : 2], ident[:])
-            dst = xg[:].bitcast(F32)[:, 512 * h : 512 * h + 512].rearrange("p (k b u) -> p k b u", k=2, u=2)
-            src = xt[:].rearrange("p (k u b) -> p k b u", k=2, u=2)
+                nc.tensor.transpose(
+                    bank[:, 128 * j : 128 * j + 128], words[:, 256 * k + u : 256 * (k + 1) : 2], ident[:]
+                )
+
+        def move_x(s, h, bank, eng):
+            dst = xg[s][:].bitcast(F32)[:, 512 * h : 512 * h + 512].rearrange("p (k b u) -> p k b u", k=2, u=2)
+            src = bank[:].rearrange("p (k u b) -> p k b u", k=2, u=2)
             if eng == "s":
                 nc.scalar.copy(out=dst, in_=src)
             else:
                 nc.vector.tensor_copy(out=dst, in_=src)
 
-        def x_tile():
-            xg = work.tile([P, 4 * 512], BF16, name="xg", align_bytes=64)
-            return xg
-
-        def x_quantize(xg):
-            xc = work.tile([P, 512], U32, name="xc", align_bytes=64)
-            xs = work.tile([P, 512], U8, name="xs", align_bytes=64)
-            nc.vector.quantize_mx(out=xc[:].bitcast(FP8X4), scales=xs[:], in_=xg[:])
-            return xc, xs
-
-        def hidden(early=False):
-            if early:
-                lv = pl.tile([P, K], F32, name="l")
-                mu = pl.tile([P, K], F32, name="l")
-            else:
-                lv = ph.tile([P, K], F32, name="h_lv")
-                mu = ph.tile([P, K], F32, name="h_mu")
-            return lv, mu
-
-        def stage1(xq, acc, groups):
-            xc, xs = xq
-            for k in groups:
-                for half in (1, 0):
-                    nc.tensor.matmul_mx(
-                        out=acc[1 - half][:],
-                        lhsT=xc[:, 128 * k : 128 * k + 128].bitcast(FP8X4),
-                        lhsT_scale=xs[:, 128 * k : 128 * k + 128],
-                        rhs=we[:, k, 1024 * half : 1024 * half + 1024].bitcast(FP4X4),
-                        rhs_scale=wes[:, k, 512 * half : 512 * half + 512],
-                        start=(k == 0),
-                        stop=(k == G1 - 1),
-                    )
-
-        def lv_bias(lv):
-            a = work.tile([P, K], F32, name="a")
-            nc.vector.tensor_tensor(a[:], lv[:], blv[:], op=ALU.add)
-            return a
-
-        def lv_exp(a):
-            e = work.tile([P, K], F32, name="e")
-            nc.scalar.activation(e[:], a[:], ACT.Exp, scale=0.5)
-            return e
-
-        def mu_gain(mu):
-            t1 = work.tile([P, K], F32, name="t1")
-            nc.vector.tensor_tensor(t1[:], mu[:], gb[:], op=ALU.mult)
-            return t1
-
-        def mu_bias(t1, eng):
-            t2 = work.tile([P, K], F32, name="t2")
-            eng.tensor_tensor(t2[:], t1[:], bmug[:], op=ALU.add)
-            return t2
-
-        def z_gain(s, e, eng):
-            w = work.tile([P, K], F32, name="w")
-            eng.tensor_tensor(w[:], e[:], epsg[:, s, :], op=ALU.mult)
-            return w
-
-        def z_sum(t2, w, eng):
-            z = work.tile([P, K], BF16, name="z")
-            eng.tensor_tensor(z[:], t2[:], w[:], op=ALU.add)
-            return z
-
-        def z_turn(z):
-            zt = px.tile([P, 256], F32, name="xt")
-            words = z[:].bitcast(F32)
-            for u in range(2):
-                nc.tensor.transpose(zt[:, 128 * u : 128 * u + 128], words[:, u:256:2], ident[:])
-            zg = work.tile([P, 512], BF16, name="zg", align_bytes=64)
-            nc.scalar.copy(
-                out=zg[:].bitcast(F32).rearrange("p (b u) -> p b u", u=2),
-                in_=zt[:].rearrange("p (u b) -> p b u", u=2),
+        def quant_x(s, h=None):
+            c = slice(0, 512) if h is None else slice(256 * h, 256 * h + 256)
+            nc.vector.quantize_mx(
+                out=xc[s][:, c].bitcast(FP8X4), scales=xs[s][:, c], in_=xg[s][:, 4 * c.start : 4 * c.stop]
             )
-            return zg
 
-        def z_quantize(zg):
-            zc = work.tile([P, P], U32, name="zc", align_bytes=64)
-            zs = work.tile([P, P], U8, name="zs", align_bytes=64)
-            nc.vector.quantize_mx(out=zc[:].bitcast(FP8X4), scales=zs[:], in_=zg[:])
-            return zc, zs
-
-        def stage2(zq):
-            zc, zs = zq
-            banks = []
-            for c in range(4):
-                acc = pl.tile([P, 512], F32, name="l")
+        def hidden(s, half, bank, ks):
+            for k in ks:
                 nc.tensor.matmul_mx(
-                    out=acc[:],
-                    lhsT=zc[:].bitcast(FP8X4),
-                    lhsT_scale=zs[:],
-                    rhs=wd[:, 1024 * c : 1024 * c + 1024].bitcast(FP4X4),
-                    rhs_scale=wds[:, 512 * c : 512 * c + 512],
-                    start=True,
-                    stop=True,
+                    out=bank[:],
+                    lhsT=xc[s][:, 128 * k : 128 * k + 128].bitcast(FP8X4),
+                    lhsT_scale=xs[s][:, 128 * k : 128 * k + 128],
+                    rhs=we[half][:, k, :].bitcast(FP4X4),
+                    rhs_scale=wes[:, k, 512 * half : 512 * half + 512],
+                    start=(k == 0),
+                    stop=(k == G1 - 1),
                 )
-                banks.append(acc)
-            return banks
 
-        def add_bias(s, c, acc):
+        def lv_bias(s, bank):
+            nc.vector.tensor_tensor(a[s][:], bank[:], blv[:], op=ALU.add)
+
+        def lv_exp(s):
+            nc.scalar.activation(e[s][:], a[s][:], ACT.Exp, scale=0.5)
+
+        def mu_gain(s, bank):
+            nc.vector.tensor_tensor(t1[s][:], bank[:], gb[:], op=ALU.mult)
+
+        def mu_bias(s, eng):
+            eng.tensor_tensor(t2[s][:], t1[s][:], bmug[:], op=ALU.add)
+
+        def eps_gain(s, eng):
+            eng.tensor_tensor(epsg[:, s, :], eps_sb[:, s, :], gb[:], op=ALU.mult)
+
+        def noise(s, eng):
+            eng.tensor_tensor(w[s][:], e[s][:], epsg[:, s, :], op=ALU.mult)
+
+        def latent(s, eng):
+            eng.tensor_tensor(z[s][:], t2[s][:], w[s][:], op=ALU.add)
+
+        def turn_z(s, bank):
+            words = z[s][:].bitcast(F32)
+            for u in range(2):
+                nc.tensor.transpose(bank[:, 128 * u : 128 * u + 128], words[:, u:256:2], ident[:])
+
+        def move_z(s, bank):
+            nc.scalar.copy(
+                out=zg[s][:].bitcast(F32).rearrange("p (b u) -> p b u", u=2),
+                in_=bank[:, 0:256].rearrange("p (u b) -> p b u", u=2),
+            )
+
+        def quant_z(s):
+            nc.vector.quantize_mx(out=zc[s][:].bitcast(FP8X4), scales=zs[s][:], in_=zg[s][:])
+
+        def decode(s, c):
+            nc.tensor.matmul_mx(
+                out=bl[c][:],
+                lhsT=zc[s][:].bitcast(FP8X4),
+                lhsT_scale=zs[s][:],
+                rhs=wd[:, 1024 * c : 1024 * c + 1024].bitcast(FP4X4),
+                rhs_scale=wds[:, 512 * c : 512 * c + 512],
+                start=True,
+                stop=True,
+            )
+
+        def add_bias(s, c):
             cols = slice(512 * c, 512 * c + 512)
-            nc.vector.tensor_tensor(l_sb[:, s, cols], acc[:], bdec[:, cols], op=ALU.add)
+            nc.vector.tensor_tensor(l_sb[:, s, cols], bl[c][:], bdec[:, cols], op=ALU.add)
 
-        NEWTON = 4
-
-        NEWTON = 4
-
-        def new_stats(s):
-            st = {}
-            for name, n in (("nm", 4), ("part", 4), ("corr", 4), ("prod", 4), ("negm", 1), ("nmc", 1), ("ssum", 1),
-                            ("sj", 1), ("y", NEWTON + 1), ("ee", NEWTON), ("nco", 1)):
-                st[name] = keep.tile([P, n], F32, name=name + str(s))
-            return st
-
-        def full_max(s, st):
-            nc.vector.tensor_reduce(st["negm"][:], l_sb[:, s, :], axis=AX.X, op=ALU.max, negate=True)
-
-        def full_exp(s, st):
-            junk = work.tile([P, J], BF16, name="junkf")
-            nc.scalar.activation(junk[:], l_sb[:, s, :], ACT.Exp, bias=st["negm"][:], accum_out=st["ssum"][:])
-
-        def half_max(s, st, h):
+        def part_max(s, i, n):
+            cols = slice(J // n * i, J // n * (i + 1))
             nc.vector.tensor_reduce(
-                st["nm"][:, h : h + 1], l_sb[:, s, 1024 * h : 1024 * h + 1024], axis=AX.X, op=ALU.max, negate=True
+                stat["nm", s][:, i : i + 1], l_sb[:, s, cols], axis=AX.X, op=ALU.max, negate=True
             )
 
-        def half_shift(st):
-            nc.vector.tensor_tensor(st["negm"][:], st["nm"][:, 0:1], st["nm"][:, 1:2], op=ALU.min)
+        def shift(s, n):
+            nc.vector.tensor_reduce(stat["negm", s][:], stat["nm", s][:, 0:n], axis=AX.X, op=ALU.min)
 
-        def part_max(s, st, c):
-            cols = slice(512 * c, 512 * c + 512)
-            nc.vector.tensor_reduce(st["nm"][:, c : c + 1], l_sb[:, s, cols], axis=AX.X, op=ALU.max, negate=True)
-
-        def part_exp(s, st, c):
-            cols = slice(512 * c, 512 * c + 512)
-            junk = work.tile([P, 512], BF16, name="junk")
+        def full_exp(s):
             nc.scalar.activation(
-                junk[:], l_sb[:, s, cols], ACT.Exp, bias=st["nm"][:, c : c + 1], accum_out=st["part"][:, c : c + 1]
+                junk[s % 2][:], l_sb[:, s, :], ACT.Exp, bias=stat["negm", s][:], accum_out=stat["ssum", s][:]
             )
 
-        def shift(st, n):
-            nc.vector.tensor_reduce(st["negm"][:], st["nm"][:, 0:n], axis=AX.X, op=ALU.min)
+        def part_exp(s, i, n):
+            cols = slice(J // n * i, J // n * (i + 1))
+            nc.scalar.activation(
+                junk[i % 2][:, 0 : J // n], l_sb[:, s, cols], ACT.Exp,
+                bias=stat["nm", s][:, i : i + 1], accum_out=stat["part", s][:, i : i + 1],
+            )
 
-        def correct(st, n):
-            nc.scalar.activation(st["corr"][:, 0:n], st["nm"][:, 0:n], ACT.Exp, scale=-1.0, bias=st["negm"][:])
+        def correct(s, n):
+            nc.scalar.activation(
+                stat["corr", s][:, 0:n], stat["nm", s][:, 0:n], ACT.Exp, scale=-1.0, bias=stat["negm", s][:]
+            )
 
-        def merge(st, n):
+        def merge(s, n):
             nc.vector.scalar_tensor_tensor(
-                st["prod"][:, 0:n], st["corr"][:, 0:n], 1.0, st["part"][:, 0:n], op0=ALU.mult, op1=ALU.mult,
-                accum_out=st["ssum"][:],
+                stat["prod", s][:, 0:n], stat["corr", s][:, 0:n], 1.0, stat["part", s][:, 0:n],
+                op0=ALU.mult, op1=ALU.mult, accum_out=stat["ssum", s][:],
             )
 
-        def half_exp(s, st, h):
-            cols = slice(1024 * h, 1024 * h + 1024)
-            junk = work.tile([P, 1024], BF16, name="junkh")
+        def log_table(s):
+            nc.scalar.activation(stat["y", s][:, 0:1], stat["ssum", s][:], ACT.Ln, scale=1.0 / J)
             nc.scalar.activation(
-                junk[:], l_sb[:, s, cols], ACT.Exp, bias=st["nm"][:, h : h + 1], accum_out=st["part"][:, h : h + 1]
+                stat["nco", s][:], stat["y", s][:, 0:1], ACT.Identity, scale=-1.0, bias=stat["negm", s][:]
             )
 
-        def log_table(st):
-            nc.scalar.activation(st["y"][:, 0:1], st["ssum"][:], ACT.Ln, scale=1.0 / J)
-            nc.scalar.activation(st["nco"][:], st["y"][:, 0:1], ACT.Identity, scale=-1.0, bias=st["negm"][:])
-
-        def guess(st):
+        def guess(s):
             nc.scalar.activation(
-                st["y"][:, 0:1], st["ssum"][:].bitcast(U32), ACT.Copy,
+                stat["y", s][:, 0:1], stat["ssum", s][:].bitcast(U32), ACT.Copy,
                 scale=LN2 * 2.0**-23, bias=-(127.0 - 0.043 + 11.0) * LN2,
             )
-            nc.scalar.activation(st["sj"][:], st["ssum"][:], ACT.Copy, scale=1.0 / J)
+            nc.scalar.activation(stat["sj", s][:], stat["ssum", s][:], ACT.Copy, scale=1.0 / J)
 
-        def newton_exp(st, i):
-            ee, y = st["ee"], st["y"]
+        def newton_exp(s, i):
+            ee, y = stat["ee", s], stat["y", s]
             if i == 0:
                 nc.scalar.activation(ee[:, 0:1], y[:, 0:1], ACT.Exp, scale=-1.0)
             else:
                 nc.scalar.activation(ee[:, i : i + 1], y[:, i : i + 1], ACT.Exp, scale=-1.0, bias=consts[:, i - 1 : i])
 
-        def newton_step(st, i):
-            ee, y = st["ee"], st["y"]
+        def newton_step(s, i):
+            ee, y = stat["ee", s], stat["y", s]
             nc.scalar.activation(
-                y[:, i + 1 : i + 2], ee[:, i : i + 1], ACT.Identity, scale=st["sj"][:], bias=y[:, i : i + 1]
+                y[:, i + 1 : i + 2], ee[:, i : i + 1], ACT.Identity, scale=stat["sj", s][:], bias=y[:, i : i + 1]
             )
 
-        def offset(st):
-            nc.scalar.activation(st["nmc"][:], st["negm"][:], ACT.Identity, bias=consts[:, NEWTON - 1 : NEWTON])
+        def offset(s):
+            nc.scalar.activation(stat["nmc", s][:], stat["negm", s][:], ACT.Identity, bias=consts[:, NEWTON - 1 : NEWTON])
             nc.scalar.activation(
-                st["nco"][:], st["y"][:, NEWTON : NEWTON + 1], ACT.Identity, scale=-1.0, bias=st["nmc"][:]
+                stat["nco", s][:], stat["y", s][:, NEWTON : NEWTON + 1], ACT.Identity,
+                scale=-1.0, bias=stat["nmc", s][:],
             )
 
-        def finish(s, st, cols, eng):
-            nco = st["nco"]
+        def finish(s, i, n, eng):
+            cols = slice(J // n * i, J // n * (i + 1))
+            nco = stat["nco", s]
             if eng == "g":
-                nc.gpsimd.tensor_scalar(o_sb[:, s, cols], l_sb[:, s, cols], 1.0, nco[:], op0=ALU.mult, op1=ALU.add)
+                nc.gpsimd.tensor_scalar(l_sb[:, s, cols], l_sb[:, s, cols], 1.0, nco[:], op0=ALU.mult, op1=ALU.add)
             elif eng == "v":
-                nc.vector.tensor_scalar(o_sb[:, s, cols], l_sb[:, s, cols], nco[:], None, op0=ALU.add)
+                nc.vector.tensor_scalar(l_sb[:, s, cols], l_sb[:, s, cols], nco[:], None, op0=ALU.add)
             else:
-                nc.scalar.activation(o_sb[:, s, cols], l_sb[:, s, cols], ACT.Identity, bias=nco[:])
+                nc.scalar.activation(l_sb[:, s, cols], l_sb[:, s, cols], ACT.Identity, bias=nco[:])
 
-        def warm_up():
-            acc = px.tile([P, 512], F32, name="xt")
-            nc.tensor.matmul(acc[:], lhsT=zeros[:, 0:P], rhs=zeros[:], start=True, stop=True)
+        def store(s, i, n):
+            cols = slice(J // n * i, J // n * (i + 1))
+            nc.sync.dma_start(out=out_v[:, s, cols], in_=l_sb[:, s, cols])
 
-        def spread(row):
-            acc = pl.tile([P, 512], F32, name="l")
-            nc.tensor.matmul(
-                acc[:], lhsT=ident_bf[:, row : row + 1].to_broadcast([P, P]), rhs=brows[:], start=True, stop=True
-            )
-            return acc
+        def early(h):
+            cols = slice(256 * h, 256 * h + 256)
+            nc.vector.tensor_copy(out=pg[:, cols, 0:2], in_=l_sb[:, 0:2, cols].rearrange("p t m -> p m t"))
 
-        def eps_gain(s, eng):
-            eng.tensor_tensor(epsg[:, s, :], eps_sb[:, s, :], gb[:], op=ALU.mult)
-
-        V, S, G = nc.vector, nc.scalar, nc.gpsimd
-        every = range(G1)
-        for i in range(4):
-            warm_up()
-        xg = x_tile()
-        x_turn(0, xg, 0, "s")
-        x_turn(0, xg, 1, "v")
-        xq0 = x_quantize(xg)
-
-        def dec_row(c, eng):
-            acc = spread(3 + c)
+        def late(c, eng):
             cols = slice(512 * c, 512 * c + 512)
+            src = l_sb[:, 2:4, cols].rearrange("p t m -> p m t")
             if eng == "s":
-                nc.scalar.copy(out=bdec[:, cols], in_=acc[:])
+                nc.scalar.copy(out=pg[:, cols, 2:4], in_=src)
             else:
-                nc.vector.tensor_copy(out=bdec[:, cols], in_=acc[:])
+                nc.vector.tensor_copy(out=pg[:, cols, 2:4], in_=src)
 
-        acc = spread(1)
-        nc.scalar.copy(out=blv[:], in_=acc[:])
-        acc = spread(2)
-        nc.vector.tensor_copy(out=gb[:], in_=acc[:])
-        acc = spread(0)
-        nc.vector.tensor_tensor(bmug[:], acc[:], gb[:], op=ALU.mult)
-        dec_row(0, "s")
-        dec_row(1, "s")
-        eps_gain(0, G)
-        h0 = hidden()
-        stage1(xq0, h0, every)
-        a = lv_bias(h0[0])
-        e0 = lv_exp(a)
-        t1 = mu_gain(h0[1])
-        xg1 = x_tile()
-        x_turn(1, xg1, 0, "s")
-        x_turn(1, xg1, 1, "v")
-        dec_row(2, "s")
-        dec_row(3, "s")
-        t2 = mu_bias(t1, V)
-        eps_gain(1, G)
-        xg2 = x_tile()
-        x_turn(2, xg2, 0, "s")
-        x_turn(2, xg2, 1, "s")
-        xq1 = x_quantize(xg1)
-        h1 = hidden(early=True)
-        stage1(xq1, h1, every[0:2])
-        w0 = z_gain(0, e0, V)
-        z = z_sum(t2, w0, V)
-        zg = z_turn(z)
-        stage1(xq1, h1, every[2:4])
-        xq = x_quantize(xg2)
-        zq = z_quantize(zg)
-        banks = stage2(zq)
-        a = lv_bias(h1[0])
-        e1 = lv_exp(a)
-        t1 = mu_gain(h1[1])
-        t2 = mu_bias(t1, G)
-        h2 = hidden()
-        stage1(xq, h2, every)
-        w = z_gain(1, e1, G)
-        z = z_sum(t2, w, G)
-        eps_gain(2, G)
-        xg3 = x_tile()
-        x_turn(3, xg3, 0, "s")
-        x_turn(3, xg3, 1, "s")
-        zg = z_turn(z)
-        warm_up()
-        warm_up()
-
-        def chain(sts, i):
-            for st in sts:
-                newton_exp(st, i)
-            for st in sts:
-                newton_step(st, i)
-
-        def finished(s, st, engs):
-            for h in range(4):
-                finish(s, st, slice(512 * h, 512 * h + 512), engs[h])
-                if h % 2:
-                    cols = slice(512 * h - 512, 512 * h + 512)
-                    nc.sync.dma_start(out=out_v[:, s, cols], in_=o_sb[:, s, cols])
-
-        sts = [new_stats(s) for s in range(T)]
-        for c in range(4):
-            add_bias(0, c, banks[c])
-        half_max(0, sts[0], 0)
-        a = lv_bias(h2[0])
-        e = lv_exp(a)
-        t1 = mu_gain(h2[1])
-        t2 = mu_bias(t1, G)
-        half_max(0, sts[0], 1)
-        half_shift(sts[0])
-        zq = z_quantize(zg)
-        xq = x_quantize(xg3)
-        banks = stage2(zq)
-        full_exp(0, sts[0])
-        w = z_gain(2, e, G)
-        z = z_sum(t2, w, G)
-        eps_gain(3, G)
-        h3 = hidden()
-        stage1(xq, h3, every)
-        zg = z_turn(z)
-        for c in range(4):
-            add_bias(1, c, banks[c])
-        a = lv_bias(h3[0])
-        e = lv_exp(a)
-        t1 = mu_gain(h3[1])
-        t2 = mu_bias(t1, G)
-        zq = z_quantize(zg)
-        banks = stage2(zq)
-        w = z_gain(3, e, G)
-        z = z_sum(t2, w, G)
-        guess(sts[0])
-        for i in range(NEWTON):
-            chain(sts[0:1], i)
-        offset(sts[0])
-        full_max(1, sts[1])
-        full_exp(1, sts[1])
-        zg = z_turn(z)
-        finished(0, sts[0], "gggg")
-        st = sts[2]
-        for c in range(4):
-            add_bias(2, c, banks[c])
-        half_max(2, st, 0)
-        zq = z_quantize(zg)
-        banks = stage2(zq)
-        guess(sts[1])
-        chain(sts[1:2], 0)
-        half_exp(2, st, 0)
-        half_max(2, st, 1)
-        for i in (1, 2, 3):
-            chain(sts[1:2], i)
-        offset(sts[1])
-        half_exp(2, st, 1)
-        shift(st, 2)
-        correct(st, 2)
-        finished(1, sts[1], "gggg")
-        st = sts[3]
-        add_bias(3, 0, banks[0])
-        add_bias(3, 1, banks[1])
-        part_max(3, st, 0)
-        add_bias(3, 2, banks[2])
-        merge(sts[2], 2)
-        part_max(3, st, 1)
-        add_bias(3, 3, banks[3])
-        part_max(3, st, 2)
-        part_max(3, st, 3)
-        part_exp(3, st, 0)
-        guess(sts[2])
-        chain(sts[2:3], 0)
-        part_exp(3, st, 1)
-        chain(sts[2:3], 1)
-        part_exp(3, st, 2)
-        chain(sts[2:3], 2)
-        part_exp(3, st, 3)
-        shift(st, 4)
-        correct(st, 4)
-        chain(sts[2:3], 3)
-        offset(sts[2])
-        prev = st
-
-        s = T - 1
-        pgs = []
-        for c in range(4):
-            pg = keep.tile([P, 512, T], BF16, name="pg" + str(c), align_bytes=64)
-            pgs.append(pg)
-
-        def early_part(h):
-            c, m = h // 2, 256 * (h % 2)
-            nc.vector.tensor_copy(
-                out=pgs[c][:, m : m + 256, 0:2],
-                in_=o_sb[:, 0:2, 512 * c + m : 512 * c + m + 256].rearrange("p t m -> p m t"),
-            )
-
-        def late_part(c):
-            cols = slice(512 * c, 512 * c + 512)
-            src = o_sb[:, 2:4, cols].rearrange("p t m -> p m t")
-            if c > 1:
-                nc.scalar.copy(out=pgs[c][:, :, 2:4], in_=src)
-            else:
-                nc.vector.tensor_copy(out=pgs[c][:, :, 2:4], in_=src)
-
-        words_v = out_1[0].rearrange("p m t -> p (m t)")
-
-        def planes(c):
+        def quant_out(c):
             cols = slice(512 * c, 512 * c + 512)
             nc.vector.quantize_mx(
-                out=pcodes[:, cols].bitcast(FP8X4),
-                scales=pscales[:, cols],
-                in_=pgs[c][:].rearrange("p m t -> p (m t)"),
+                out=pcodes[:, cols].bitcast(FP8X4), scales=pscales[:, cols],
+                in_=pg[:, cols, :].rearrange("p m t -> p (m t)"),
             )
+
+        def store_words(c):
+            cols = slice(512 * c, 512 * c + 512)
             nc.sync.dma_start(
                 out=words_v[:, 2048 * c : 2048 * c + 2048].bitcast(I32), in_=pcodes[:, cols].bitcast(I32)
             )
 
-        for h in range(3):
-            early_part(h)
-        merge(prev, 4)
-        log_table(prev)
-        for h in range(3, 5):
-            early_part(h)
-        finished(2, sts[2], "vvvv")
-        for h in range(5, 8):
-            early_part(h)
-        for c in (0, 1, 3, 2):
-            cols = slice(512 * c, 512 * c + 512)
-            finish(s, prev, cols, "vsss"[c])
-            nc.sync.dma_start(out=out_v[:, s, cols], in_=o_sb[:, s, cols])
-        for c in (0, 1, 3, 2):
-            late_part(c)
-        for c in (0, 1, 3, 2):
-            planes(c)
-        for q in range(4):
+        def store_scales(q):
             nc.sync.dma_start(
                 out=out_2[0, 4 * q : 4 * q + 4, :].bitcast(I32), in_=pscales[32 * q : 32 * q + 4, :].bitcast(I32)
             )
+
+        V.memset(zeros[:], 0.0)
+        V.memset(rows_h[:], 0.0)
+        V.memset(wes_w, 0)
+        S.dma_start(out=rows_h[0:2, :], in_=b_enc.rearrange("(c n) -> c n", c=2))
+        V.memset(rows_g[:], 0.0)
+        V.memset(warm[:], 0.0)
+        V.memset(wds[:].bitcast(I32), 0)
+        V.memset(rows_d[:], 0.0)
+        make_identity(nc, ident[:])
+        G.memset(consts[:, 0:1], 1.0)
+        G.memset(consts[:, 1:2], 2.0)
+        G.memset(consts[:, 2:3], 3.0)
+        G.memset(consts[:, 3:4], 4.0)
+        S.activation(warm[:, 1:2], warm[:, 0:1], ACT.Exp)
+        V.tensor_copy(out=ident_bf[:], in_=ident[:])
+        nc.sync.dma_start(out=x_sb[:, 0, 0:1024], in_=x_v[:, 0, 0:1024])
+        nc.sync.dma_start(out=x_sb[:, 0, 1024:2048], in_=x_v[:, 0, 1024:2048])
+        load_wes(0)
+        load_wes(1)
+        load_wes(2)
+        load_wes(3)
+        load_w(1)
+        nc.sync.dma_start(out=rows_g[0:1, :], in_=g.rearrange("(c n) -> c n", c=1))
+        load_w(0)
+        nc.sync.dma_start(out=x_sb[:, 1, :], in_=x_v[:, 1, :])
+        nc.sync.dma_start(out=eps_sb[:, 0:2, :], in_=eps_v[:, 0:2, :])
+        nc.sync.dma_start(out=rows_d[0:4, :], in_=b_dec.rearrange("(c n) -> c n", c=4))
+        nc.sync.dma_start(out=x_sb[:, 2, :], in_=x_v[:, 2, :])
+        load_wds(0)
+        load_wds(1)
+        load_wds(2)
+        load_wds(3)
+        nc.sync.dma_start(out=wd[:].bitcast(I32), in_=w_dec_words[0].bitcast(I32))
+        nc.sync.dma_start(out=x_sb[:, 3, :], in_=x_v[:, 3, :])
+        nc.sync.dma_start(out=eps_sb[:, 2:4, :], in_=eps_v[:, 2:4, :])
+        warm_up(bx[1])
+        warm_up(bx[0])
+        warm_up(bx[0])
+        warm_up(bx[0])
+        turn_x(0, 0, bx[0])
+        spread(rows_h, 1, bl[0])
+        warm_up(bx[1])
+        spread(rows_h, 0, bl[2])
+        warm_up(bx[1])
+        turn_x(0, 1, bx[1])
+        move_x(0, 0, bx[0], "s")
+        quant_x(0, 0)
+        move_x(0, 1, bx[1], "v")
+        quant_x(0, 1)
+        spread(rows_g, 0, bl[1])
+        hidden(0, 1, bh[0], (0, 1))
+        hidden(0, 1, bh[0], (2, 3))
+        S.copy(out=bmu[:], in_=bl[2][:])
+        S.copy(out=gb[:], in_=bl[1][:])
+        S.copy(out=blv[:], in_=bl[0][:])
+        hidden(0, 0, bh[1], (0, 1))
+        hidden(0, 0, bh[1], (2, 3))
+        turn_x(1, 1, bx[1])
+        turn_x(1, 0, bx[0])
+        spread(rows_d, 1, bl[1])
+        spread(rows_d, 0, bl[0])
+        G.tensor_tensor(bmug[:], bmu[:], gb[:], op=ALU.mult)
+        eps_gain(0, G)
+        eps_gain(1, G)
+        lv_bias(0, bh[0])
+        mu_gain(0, bh[1])
+        lv_exp(0)
+        move_x(1, 1, bx[1], "s")
+        move_x(1, 0, bx[0], "s")
+        turn_x(2, 1, bx[1])
+        turn_x(2, 0, bx[0])
+        mu_bias(0, V)
+        noise(0, V)
+        quant_x(1)
+        S.copy(out=bdec[:, 0:512], in_=bl[0][:])
+        S.copy(out=bdec[:, 512:1024], in_=bl[1][:])
+        move_x(2, 0, bx[0], "s")
+        latent(0, V)
+        spread(rows_d, 2, bl[0])
+        hidden(1, 1, bl[2], (0, 1))
+        hidden(1, 1, bl[2], (2, 3))
+        turn_z(0, bx[0])
+        hidden(1, 0, bl[3], (0, 1))
+        hidden(1, 0, bl[3], (2, 3))
+        spread(rows_d, 3, bl[1])
+        S.copy(out=bdec[:, 1024:1536], in_=bl[0][:])
+        move_x(2, 1, bx[1], "s")
+        move_z(0, bx[0])
+        lv_bias(1, bl[2])
+        quant_x(2)
+        quant_z(0)
+        mu_gain(1, bl[3])
+        lv_exp(1)
+        S.copy(out=bdec[:, 1536:2048], in_=bl[1][:])
+        noise(1, V)
+        mu_bias(1, G)
+        eps_gain(2, G)
+        latent(1, G)
+        turn_x(3, 0, bx[0])
+        decode(0, 0)
+        decode(0, 3)
+        decode(0, 2)
+        decode(0, 1)
+        hidden(2, 0, bh[1], (0, 1))
+        hidden(2, 0, bh[1], (2, 3))
+        hidden(2, 1, bh[0], (0, 1))
+        turn_x(3, 1, bx[1])
+        move_x(3, 0, bx[0], "s")
+        move_x(3, 1, bx[1], "s")
+        hidden(2, 1, bh[0], (2, 3))
+        turn_z(1, bx[0])
+        warm_up(bx[1])
+        add_bias(0, 0)
+        add_bias(0, 3)
+        add_bias(0, 2)
+        add_bias(0, 1)
+        mu_gain(2, bh[1])
+        part_max(0, 1, 2)
+        lv_bias(2, bh[0])
+        part_max(0, 0, 2)
+        move_z(1, bx[0])
+        lv_exp(2)
+        quant_z(1)
+        quant_x(3)
+        noise(2, V)
+        shift(0, 2)
+        decode(1, 3)
+        full_exp(0)
+        mu_bias(2, G)
+        latent(2, G)
+        eps_gain(3, G)
+        decode(1, 0)
+        decode(1, 1)
+        decode(1, 2)
+        hidden(3, 1, bh[0], (0, 1))
+        warm_up(bx[1])
+        hidden(3, 1, bh[0], (2, 3))
+        hidden(3, 0, bh[1], (0, 1))
+        turn_z(2, bx[1])
+        hidden(3, 0, bh[1], (2, 3))
+        add_bias(1, 3)
+        add_bias(1, 0)
+        add_bias(1, 1)
+        add_bias(1, 2)
+        lv_bias(3, bh[0])
+        part_max(1, 1, 2)
+        move_z(2, bx[1])
+        lv_exp(3)
+        guess(0)
+        newton_exp(0, 0)
+        newton_step(0, 0)
+        newton_exp(0, 1)
+        newton_step(0, 1)
+        newton_exp(0, 2)
+        mu_gain(3, bh[1])
+        quant_z(2)
+        decode(2, 0)
+        decode(2, 2)
+        decode(2, 3)
+        decode(2, 1)
+        part_max(1, 0, 2)
+        shift(1, 2)
+        noise(3, V)
+        mu_bias(3, G)
+        latent(3, G)
+        add_bias(2, 0)
+        add_bias(2, 1)
+        add_bias(2, 2)
+        part_max(2, 0, 2)
+        add_bias(2, 3)
+        turn_z(3, bx[0])
+        newton_step(0, 2)
+        full_exp(1)
+        newton_exp(0, 3)
+        guess(1)
+        newton_step(0, 3)
+        newton_exp(1, 0)
+        move_z(3, bx[0])
+        newton_step(1, 0)
+        newton_exp(1, 1)
+        offset(0)
+        newton_step(1, 1)
+        finish(0, 2, 4, "g")
+        finish(0, 1, 4, "g")
+        finish(0, 3, 4, "g")
+        finish(0, 0, 4, "g")
+        store(0, 0, 1)
+        quant_z(3)
+        part_max(2, 1, 2)
+        decode(3, 1)
+        decode(3, 0)
+        decode(3, 3)
+        decode(3, 2)
+        part_exp(2, 0, 2)
+        newton_exp(1, 2)
+        add_bias(3, 1)
+        add_bias(3, 0)
+        shift(2, 2)
+        newton_step(1, 2)
+        part_exp(2, 1, 2)
+        newton_exp(1, 3)
+        correct(2, 2)
+        newton_step(1, 3)
+        offset(1)
+        finish(1, 2, 4, "g")
+        finish(1, 1, 4, "g")
+        finish(1, 0, 4, "g")
+        finish(1, 3, 4, "g")
+        store(1, 0, 1)
+        part_max(3, 0, 4)
+        merge(2, 2)
+        add_bias(3, 3)
+        part_max(3, 1, 4)
+        add_bias(3, 2)
+        part_max(3, 2, 4)
+        part_max(3, 3, 4)
+        guess(2)
+        newton_exp(2, 0)
+        newton_step(2, 0)
+        newton_exp(2, 1)
+        part_exp(3, 0, 4)
+        newton_step(2, 1)
+        part_exp(3, 1, 4)
+        newton_exp(2, 2)
+        early(4)
+        early(6)
+        shift(3, 4)
+        early(7)
+        early(3)
+        newton_step(2, 2)
+        part_exp(3, 2, 4)
+        newton_exp(2, 3)
+        part_exp(3, 3, 4)
+        newton_step(2, 3)
+        offset(2)
+        correct(3, 4)
+        finish(2, 1, 4, "v")
+        finish(2, 0, 4, "v")
+        merge(3, 4)
+        finish(2, 3, 4, "v")
+        early(1)
+        finish(2, 2, 4, "v")
+        early(2)
+        log_table(3)
+        store(2, 0, 2)
+        finish(3, 0, 4, "v")
+        store(2, 1, 2)
+        finish(3, 3, 4, "s")
+        finish(3, 1, 4, "s")
+        finish(3, 2, 4, "s")
+        store(3, 0, 4)
+        store(3, 1, 4)
+        store(3, 3, 4)
+        store(3, 2, 4)
+        early(0)
+        late(0, "v")
+        late(1, "v")
+        quant_out(0)
+        quant_out(1)
+        early(5)
+        late(3, "s")
+        late(2, "s")
+        store_words(0)
+        quant_out(3)
+        quant_out(2)
+        store_words(1)
+        store_words(3)
+        store_words(2)
+        store_scales(0)
+        store_scales(1)
+        store_scales(2)
+        store_scales(3)

@@ -54,6 +54,7 @@ def tile_multvaereparamitemloglift_x2_kernel(
         blv = sb("blv", [P, K], F32)
         gb = sb("gb", [P, K], BF16)
         bmu = sb("bmu", [P, K], BF16)
+        tmp = [sb("tmp" + str(i), [P, 512], F32) for i in range(2)]
         bmug = sb("bmug", [P, K], F32)
         bdec = sb("bdec", [P, J], BF16)
         epsg = sb("epsg", [P, T, K], F32)
@@ -199,6 +200,13 @@ def tile_multvaereparamitemloglift_x2_kernel(
             cols = slice(512 * c, 512 * c + 512)
             nc.vector.tensor_tensor(l_sb[:, s, cols], bl[c][:], bdec[:, cols], op=ALU.add)
 
+        def drain(s, c):
+            nc.scalar.copy(out=tmp[s % 2][:], in_=bl[c][:])
+
+        def add_away(s, c):
+            cols = slice(512 * c, 512 * c + 512)
+            nc.gpsimd.tensor_tensor(l_sb[:, s, cols], tmp[s % 2][:], bdec[:, cols], op=ALU.add)
+
         def part_max(s, i, n):
             cols = slice(J // n * i, J // n * (i + 1))
             nc.vector.tensor_reduce(
@@ -233,6 +241,8 @@ def tile_multvaereparamitemloglift_x2_kernel(
 
         def log_table(s):
             nc.scalar.activation(stat["y", s][:, 0:1], stat["ssum", s][:], ACT.Ln, scale=1.0 / J)
+
+        def log_offset(s):
             nc.scalar.activation(
                 stat["nco", s][:], stat["y", s][:, 0:1], ACT.Identity, scale=-1.0, bias=stat["negm", s][:]
             )
@@ -274,6 +284,13 @@ def tile_multvaereparamitemloglift_x2_kernel(
             else:
                 nc.scalar.activation(l_sb[:, s, cols], l_sb[:, s, cols], ACT.Identity, bias=nco[:])
 
+        def finish_first(s, i, n):
+            cols = slice(J // n * i, J // n * (i + 1))
+            nc.vector.tensor_scalar(
+                l_sb[:, s, cols], l_sb[:, s, cols], stat["y", s][:, 0:1], stat["negm", s][:],
+                op0=ALU.subtract, op1=ALU.add,
+            )
+
         def store(s, i, n):
             cols = slice(J // n * i, J // n * (i + 1))
             nc.sync.dma_start(out=out_v[:, s, cols], in_=l_sb[:, s, cols])
@@ -304,7 +321,7 @@ def tile_multvaereparamitemloglift_x2_kernel(
             )
 
         def store_scales(q):
-            nc.sync.dma_start(
+            nc.scalar.dma_start(
                 out=out_2[0, 4 * q : 4 * q + 4, :].bitcast(I32), in_=pscales[32 * q : 32 * q + 4, :].bitcast(I32)
             )
 
@@ -343,32 +360,32 @@ def tile_multvaereparamitemloglift_x2_kernel(
         nc.sync.dma_start(out=wd[:].bitcast(I32), in_=w_dec_words[0].bitcast(I32))
         nc.sync.dma_start(out=x_sb[:, 3, :], in_=x_v[:, 3, :])
         nc.sync.dma_start(out=eps_sb[:, 2:4, :], in_=eps_v[:, 2:4, :])
+        warm_up(bx[0])
         warm_up(bx[1])
         warm_up(bx[0])
-        warm_up(bx[0])
+        warm_up(bx[1])
         warm_up(bx[0])
         turn_x(0, 0, bx[0])
         spread(rows_h, 1, bl[0])
         warm_up(bx[1])
         spread(rows_h, 0, bl[2])
-        warm_up(bx[1])
         turn_x(0, 1, bx[1])
         move_x(0, 0, bx[0], "s")
+        S.copy(out=bmu[:], in_=bl[2][:])
+        S.copy(out=blv[:], in_=bl[0][:])
         quant_x(0, 0)
         move_x(0, 1, bx[1], "v")
         quant_x(0, 1)
         spread(rows_g, 0, bl[1])
         hidden(0, 1, bh[0], (0, 1))
         hidden(0, 1, bh[0], (2, 3))
-        S.copy(out=bmu[:], in_=bl[2][:])
         S.copy(out=gb[:], in_=bl[1][:])
-        S.copy(out=blv[:], in_=bl[0][:])
         hidden(0, 0, bh[1], (0, 1))
         hidden(0, 0, bh[1], (2, 3))
         turn_x(1, 1, bx[1])
         turn_x(1, 0, bx[0])
-        spread(rows_d, 1, bl[1])
         spread(rows_d, 0, bl[0])
+        spread(rows_d, 1, bl[1])
         G.tensor_tensor(bmug[:], bmu[:], gb[:], op=ALU.mult)
         eps_gain(0, G)
         eps_gain(1, G)
@@ -384,90 +401,90 @@ def tile_multvaereparamitemloglift_x2_kernel(
         quant_x(1)
         S.copy(out=bdec[:, 0:512], in_=bl[0][:])
         S.copy(out=bdec[:, 512:1024], in_=bl[1][:])
+        move_x(2, 1, bx[1], "s")
         move_x(2, 0, bx[0], "s")
         latent(0, V)
         spread(rows_d, 2, bl[0])
+        spread(rows_d, 3, bl[1])
         hidden(1, 1, bl[2], (0, 1))
         hidden(1, 1, bl[2], (2, 3))
         turn_z(0, bx[0])
         hidden(1, 0, bl[3], (0, 1))
         hidden(1, 0, bl[3], (2, 3))
-        spread(rows_d, 3, bl[1])
         S.copy(out=bdec[:, 1024:1536], in_=bl[0][:])
-        move_x(2, 1, bx[1], "s")
+        S.copy(out=bdec[:, 1536:2048], in_=bl[1][:])
         move_z(0, bx[0])
         lv_bias(1, bl[2])
         quant_x(2)
         quant_z(0)
         mu_gain(1, bl[3])
         lv_exp(1)
-        S.copy(out=bdec[:, 1536:2048], in_=bl[1][:])
         noise(1, V)
         mu_bias(1, G)
         eps_gain(2, G)
         latent(1, G)
         turn_x(3, 0, bx[0])
         decode(0, 0)
-        decode(0, 3)
         decode(0, 2)
         decode(0, 1)
         hidden(2, 0, bh[1], (0, 1))
+        decode(0, 3)
         hidden(2, 0, bh[1], (2, 3))
-        hidden(2, 1, bh[0], (0, 1))
         turn_x(3, 1, bx[1])
-        move_x(3, 0, bx[0], "s")
-        move_x(3, 1, bx[1], "s")
+        hidden(2, 1, bh[0], (0, 1))
         hidden(2, 1, bh[0], (2, 3))
-        turn_z(1, bx[0])
+        move_x(3, 1, bx[1], "s")
+        move_x(3, 0, bx[0], "s")
         warm_up(bx[1])
+        turn_z(1, bx[0])
         add_bias(0, 0)
-        add_bias(0, 3)
-        add_bias(0, 2)
         add_bias(0, 1)
-        mu_gain(2, bh[1])
-        part_max(0, 1, 2)
-        lv_bias(2, bh[0])
+        add_bias(0, 2)
         part_max(0, 0, 2)
+        add_bias(0, 3)
+        mu_gain(2, bh[1])
+        lv_bias(2, bh[0])
+        part_max(0, 1, 2)
         move_z(1, bx[0])
         lv_exp(2)
         quant_z(1)
         quant_x(3)
         noise(2, V)
         shift(0, 2)
+        warm_up(bx[1])
+        decode(1, 2)
+        decode(1, 0)
         decode(1, 3)
-        full_exp(0)
+        decode(1, 1)
         mu_bias(2, G)
         latent(2, G)
+        drain(1, 0)
+        full_exp(0)
+        add_away(1, 0)
         eps_gain(3, G)
-        decode(1, 0)
-        decode(1, 1)
-        decode(1, 2)
-        hidden(3, 1, bh[0], (0, 1))
-        warm_up(bx[1])
-        hidden(3, 1, bh[0], (2, 3))
         hidden(3, 0, bh[1], (0, 1))
+        hidden(3, 1, bh[0], (0, 1))
+        hidden(3, 1, bh[0], (2, 3))
         turn_z(2, bx[1])
         hidden(3, 0, bh[1], (2, 3))
-        add_bias(1, 3)
-        add_bias(1, 0)
-        add_bias(1, 1)
         add_bias(1, 2)
-        lv_bias(3, bh[0])
+        add_bias(1, 3)
+        add_bias(1, 1)
         part_max(1, 1, 2)
+        lv_bias(3, bh[0])
         move_z(2, bx[1])
-        lv_exp(3)
         guess(0)
+        lv_exp(3)
         newton_exp(0, 0)
         newton_step(0, 0)
         newton_exp(0, 1)
         newton_step(0, 1)
-        newton_exp(0, 2)
         mu_gain(3, bh[1])
         quant_z(2)
         decode(2, 0)
-        decode(2, 2)
-        decode(2, 3)
         decode(2, 1)
+        decode(2, 3)
+        decode(2, 2)
         part_max(1, 0, 2)
         shift(1, 2)
         noise(3, V)
@@ -475,102 +492,104 @@ def tile_multvaereparamitemloglift_x2_kernel(
         latent(3, G)
         add_bias(2, 0)
         add_bias(2, 1)
+        add_bias(2, 3)
         add_bias(2, 2)
         part_max(2, 0, 2)
-        add_bias(2, 3)
         turn_z(3, bx[0])
-        newton_step(0, 2)
+        newton_exp(0, 2)
         full_exp(1)
-        newton_exp(0, 3)
+        newton_step(0, 2)
         guess(1)
-        newton_step(0, 3)
+        newton_exp(0, 3)
         newton_exp(1, 0)
         move_z(3, bx[0])
         newton_step(1, 0)
+        newton_step(0, 3)
         newton_exp(1, 1)
         offset(0)
         newton_step(1, 1)
-        finish(0, 2, 4, "g")
-        finish(0, 1, 4, "g")
-        finish(0, 3, 4, "g")
         finish(0, 0, 4, "g")
+        finish(0, 1, 4, "g")
+        finish(0, 2, 4, "g")
+        finish(0, 3, 4, "g")
         store(0, 0, 1)
         quant_z(3)
         part_max(2, 1, 2)
-        decode(3, 1)
         decode(3, 0)
         decode(3, 3)
         decode(3, 2)
-        part_exp(2, 0, 2)
+        decode(3, 1)
         newton_exp(1, 2)
-        add_bias(3, 1)
+        part_exp(2, 0, 2)
         add_bias(3, 0)
         shift(2, 2)
+        add_bias(3, 3)
         newton_step(1, 2)
         part_exp(2, 1, 2)
         newton_exp(1, 3)
         correct(2, 2)
         newton_step(1, 3)
         offset(1)
-        finish(1, 2, 4, "g")
         finish(1, 1, 4, "g")
         finish(1, 0, 4, "g")
         finish(1, 3, 4, "g")
+        finish(1, 2, 4, "g")
         store(1, 0, 1)
         part_max(3, 0, 4)
         merge(2, 2)
-        add_bias(3, 3)
+        add_bias(3, 1)
+        part_max(3, 3, 4)
         part_max(3, 1, 4)
         add_bias(3, 2)
-        part_max(3, 2, 4)
-        part_max(3, 3, 4)
         guess(2)
+        part_max(3, 2, 4)
+        early(0)
+        early(5)
+        shift(3, 4)
+        early(2)
         newton_exp(2, 0)
         newton_step(2, 0)
         newton_exp(2, 1)
         part_exp(3, 0, 4)
         newton_step(2, 1)
-        part_exp(3, 1, 4)
         newton_exp(2, 2)
-        early(4)
-        early(6)
-        shift(3, 4)
-        early(7)
-        early(3)
+        part_exp(3, 1, 4)
         newton_step(2, 2)
-        part_exp(3, 2, 4)
         newton_exp(2, 3)
         part_exp(3, 3, 4)
         newton_step(2, 3)
         offset(2)
+        part_exp(3, 2, 4)
         correct(3, 4)
         finish(2, 1, 4, "v")
         finish(2, 0, 4, "v")
-        merge(3, 4)
         finish(2, 3, 4, "v")
-        early(1)
+        early(4)
+        merge(3, 4)
         finish(2, 2, 4, "v")
-        early(2)
+        early(6)
+        early(7)
         log_table(3)
+        log_offset(3)
         store(2, 0, 2)
-        finish(3, 0, 4, "v")
+        finish_first(3, 0, 4)
+        early(3)
+        late(0, "v")
+        early(1)
         store(2, 1, 2)
-        finish(3, 3, 4, "s")
         finish(3, 1, 4, "s")
+        finish(3, 3, 4, "s")
         finish(3, 2, 4, "s")
         store(3, 0, 4)
         store(3, 1, 4)
         store(3, 3, 4)
         store(3, 2, 4)
-        early(0)
-        late(0, "v")
         late(1, "v")
         quant_out(0)
-        quant_out(1)
-        early(5)
         late(3, "s")
         late(2, "s")
         store_words(0)
+        quant_out(1)
         quant_out(3)
         quant_out(2)
         store_words(1)

from contextlib import ExitStack

import concourse.mybir as mybir
from concourse.masks import make_identity

F32 = mybir.dt.float32
BF16 = mybir.dt.bfloat16
I32 = mybir.dt.int32
U32 = mybir.dt.uint32
U8 = mybir.dt.uint8
FP8X4 = mybir.dt.float8_e4m3fn_x4
FP4X4 = mybir.dt.float4_e2m1fn_x4
ALU = mybir.AluOpType
ACT = mybir.ActivationFunctionType
AX = mybir.AxisListType

P = 128
B, I, K, J = 512, 2048, 512, 2048
T = 4
G1 = I // 512
NEWTON = 4
FLOPS = 2 * B * I * 2 * K + 2 * B * K * J
LN2 = 0.6931471805599453
LNJ = 7.6246189861593985


def tile_multvaereparamitemloglift_x2_kernel(
    tc, x, w_enc_words, w_enc_scales, b_enc, eps, g, w_dec_words, w_dec_scales, b_dec, out_0, out_1, out_2
):
    nc = tc.nc
    V, S, G = nc.vector, nc.scalar, nc.gpsimd
    with ExitStack() as ctx:
        keep = ctx.enter_context(tc.tile_pool(name="keep", bufs=1))
        banks = ctx.enter_context(tc.psum_pool(name="banks", bufs=1))
        ctx.enter_context(tc.manual_schedule())

        def sb(name, shape, dtype, align=64):
            return keep.tile(shape, dtype, name=name, align_bytes=align)

        x_sb = sb("x_sb", [P, T, I], BF16)
        we = [sb("we" + str(i), [P, G1, 2 * K], U8) for i in range(2)]
        wes = sb("wes", [P, G1, 2 * K], U8)
        wd = sb("wd", [P, 2 * J], U8)
        wds = sb("wds", [P, J], U8)
        eps_sb = sb("eps_sb", [P, T, K], BF16)
        zeros = sb("zeros", [P, 512], BF16)
        rows_h = sb("rows_h", [P, 512], BF16)
        rows_g = sb("rows_g", [P, 512], BF16)
        rows_d = sb("rows_d", [P, 512], BF16)
        ident = sb("ident", [P, P], F32)
        ident_bf = sb("ident_bf", [P, P], BF16)
        consts = sb("consts", [P, NEWTON], F32)
        warm = sb("warm", [P, 2], F32)
        blv = sb("blv", [P, K], F32)
        gb = sb("gb", [P, K], BF16)
        bmu = sb("bmu", [P, K], BF16)
        tmp = [sb("tmp" + str(i), [P, 512], F32) for i in range(2)]
        bmug = sb("bmug", [P, K], F32)
        bdec = sb("bdec", [P, J], BF16)
        epsg = sb("epsg", [P, T, K], F32)
        l_sb = sb("l_sb", [P, T, J], F32)
        pcodes = sb("pcodes", [P, J], U32)
        pscales = sb("pscales", [P, J], U8)
        pg = sb("pg", [P, J, T], BF16)
        xg = [sb("xg" + str(s), [P, 2048], BF16) for s in range(3)]
        xg.append(xg[0])
        xc = [sb("xc" + str(s), [P, 512], U32) for s in range(T)]
        xs = [sb("xs" + str(s), [P, 512], U8) for s in range(T)]
        a = [sb("a" + str(s), [P, K], F32) for s in range(T)]
        e = [sb("e" + str(s), [P, K], F32) for s in range(T)]
        t1 = [sb("t1" + str(s), [P, K], F32) for s in range(T)]
        t2 = [sb("t2" + str(s), [P, K], F32) for s in range(T)]
        w = [sb("w" + str(s), [P, K], F32) for s in range(T)]
        z = [sb("z" + str(s), [P, K], BF16) for s in range(T)]
        zg = [sb("zg" + str(s), [P, 512], BF16) for s in range(T)]
        zc = [sb("zc" + str(s), [P, P], U32) for s in range(T)]
        zs = [sb("zs" + str(s), [P, P], U8) for s in range(T)]
        junk = [sb("junk" + str(s), [P, J], BF16) for s in range(2)]
        stat = {}
        for s in range(T):
            for name, n in (("nm", 4), ("part", 4), ("corr", 4), ("prod", 4), ("negm", 1), ("nmc", 1), ("ssum", 1),
                            ("sj", 1), ("y", NEWTON + 1), ("ee", NEWTON), ("nco", 1)):
                stat[name, s] = sb(name + str(s), [P, n], F32, 32)
        bx = [banks.tile([P, 512], F32, name="bx" + str(i)) for i in range(2)]
        bh = [banks.tile([P, 512], F32, name="bh" + str(i)) for i in range(2)]
        bl = [banks.tile([P, 512], F32, name="bl" + str(i)) for i in range(4)]

        x_v = x.rearrange("(p t) k -> p t k", t=T)
        eps_v = eps.rearrange("(p t) k -> p t k", t=T)
        out_v = out_0.rearrange("(p t) m -> p t m", t=T)
        words_v = out_1[0].rearrange("p m t -> p (m t)")
        wes_w = wes[:].rearrange("p g n -> p (g n)").bitcast(I32)

        def load_w(half):
            cols = slice(1024 * half, 1024 * half + 1024)
            nc.sync.dma_start(
                out=we[half][:].bitcast(I32), in_=w_enc_words[:, :, cols].rearrange("g p n -> p g n").bitcast(I32)
            )

        def load_wes(q):
            nc.sync.dma_start(
                out=wes[32 * q : 32 * q + 4].bitcast(I32),
                in_=w_enc_scales[:, 4 * q : 4 * q + 4, :].rearrange("g q n -> q g n").bitcast(I32),
            )

        def load_wds(q):
            nc.sync.dma_start(
                out=wds[32 * q : 32 * q + 4, :].bitcast(I32), in_=w_dec_scales[0, 4 * q : 4 * q + 4, :].bitcast(I32)
            )

        def warm_up(bank):
            nc.tensor.matmul(bank[:], lhsT=zeros[:, 0:P], rhs=zeros[:], start=True, stop=True)

        def spread(rows, row, bank):
            nc.tensor.matmul(
                bank[:], lhsT=ident_bf[:, row : row + 1].to_broadcast([P, P]), rhs=rows[:], start=True, stop=True
            )

        def turn_x(s, h, bank):
            words = x_sb[:, s, :].bitcast(F32)
            for j in range(4):
                k, u = 2 * h + j // 2, j % 2
                nc.tensor.transpose(
                    bank[:, 128 * j : 128 * j + 128], words[:, 256 * k + u : 256 * (k + 1) : 2], ident[:]
                )

        def move_x(s, h, bank, eng):
            dst = xg[s][:].bitcast(F32)[:, 512 * h : 512 * h + 512].rearrange("p (k b u) -> p k b u", k=2, u=2)
            src = bank[:].rearrange("p (k u b) -> p k b u", k=2, u=2)
            if eng == "s":
                nc.scalar.copy(out=dst, in_=src)
            else:
                nc.vector.tensor_copy(out=dst, in_=src)

        def quant_x(s, h=None):
            c = slice(0, 512) if h is None else slice(256 * h, 256 * h + 256)
            nc.vector.quantize_mx(
                out=xc[s][:, c].bitcast(FP8X4), scales=xs[s][:, c], in_=xg[s][:, 4 * c.start : 4 * c.stop]
            )

        def hidden(s, half, bank, ks):
            for k in ks:
                nc.tensor.matmul_mx(
                    out=bank[:],
                    lhsT=xc[s][:, 128 * k : 128 * k + 128].bitcast(FP8X4),
                    lhsT_scale=xs[s][:, 128 * k : 128 * k + 128],
                    rhs=we[half][:, k, :].bitcast(FP4X4),
                    rhs_scale=wes[:, k, 512 * half : 512 * half + 512],
                    start=(k == 0),
                    stop=(k == G1 - 1),
                )

        def lv_bias(s, bank):
            nc.vector.tensor_tensor(a[s][:], bank[:], blv[:], op=ALU.add)

        def lv_exp(s):
            nc.scalar.activation(e[s][:], a[s][:], ACT.Exp, scale=0.5)

        def mu_gain(s, bank):
            nc.vector.tensor_tensor(t1[s][:], bank[:], gb[:], op=ALU.mult)

        def mu_bias(s, eng):
            eng.tensor_tensor(t2[s][:], t1[s][:], bmug[:], op=ALU.add)

        def eps_gain(s, eng):
            eng.tensor_tensor(epsg[:, s, :], eps_sb[:, s, :], gb[:], op=ALU.mult)

        def noise(s, eng):
            eng.tensor_tensor(w[s][:], e[s][:], epsg[:, s, :], op=ALU.mult)

        def latent(s, eng):
            eng.tensor_tensor(z[s][:], t2[s][:], w[s][:], op=ALU.add)

        def turn_z(s, bank):
            words = z[s][:].bitcast(F32)
            for u in range(2):
                nc.tensor.transpose(bank[:, 128 * u : 128 * u + 128], words[:, u:256:2], ident[:])

        def move_z(s, bank):
            nc.scalar.copy(
                out=zg[s][:].bitcast(F32).rearrange("p (b u) -> p b u", u=2),
                in_=bank[:, 0:256].rearrange("p (u b) -> p b u", u=2),
            )

        def quant_z(s):
            nc.vector.quantize_mx(out=zc[s][:].bitcast(FP8X4), scales=zs[s][:], in_=zg[s][:])

        def decode(s, c):
            nc.tensor.matmul_mx(
                out=bl[c][:],
                lhsT=zc[s][:].bitcast(FP8X4),
                lhsT_scale=zs[s][:],
                rhs=wd[:, 1024 * c : 1024 * c + 1024].bitcast(FP4X4),
                rhs_scale=wds[:, 512 * c : 512 * c + 512],
                start=True,
                stop=True,
            )

        def add_bias(s, c):
            cols = slice(512 * c, 512 * c + 512)
            nc.vector.tensor_tensor(l_sb[:, s, cols], bl[c][:], bdec[:, cols], op=ALU.add)

        def drain(s, c):
            nc.scalar.copy(out=tmp[s % 2][:], in_=bl[c][:])

        def add_away(s, c):
            cols = slice(512 * c, 512 * c + 512)
            nc.gpsimd.tensor_tensor(l_sb[:, s, cols], tmp[s % 2][:], bdec[:, cols], op=ALU.add)

        def part_max(s, i, n):
            cols = slice(J // n * i, J // n * (i + 1))
            nc.vector.tensor_reduce(
                stat["nm", s][:, i : i + 1], l_sb[:, s, cols], axis=AX.X, op=ALU.max, negate=True
            )

        def shift(s, n):
            nc.vector.tensor_reduce(stat["negm", s][:], stat["nm", s][:, 0:n], axis=AX.X, op=ALU.min)

        def full_exp(s):
            nc.scalar.activation(
                junk[s % 2][:], l_sb[:, s, :], ACT.Exp, bias=stat["negm", s][:], accum_out=stat["ssum", s][:]
            )

        def part_exp(s, i, n):
            cols = slice(J // n * i, J // n * (i + 1))
            nc.scalar.activation(
                junk[i % 2][:, 0 : J // n], l_sb[:, s, cols], ACT.Exp,
                bias=stat["nm", s][:, i : i + 1], accum_out=stat["part", s][:, i : i + 1],
            )

        def correct(s, n):
            nc.scalar.activation(
                stat["corr", s][:, 0:n], stat["nm", s][:, 0:n], ACT.Exp, scale=-1.0, bias=stat["negm", s][:]
            )

        def merge(s, n):
            nc.vector.scalar_tensor_tensor(
                stat["prod", s][:, 0:n], stat["corr", s][:, 0:n], 1.0, stat["part", s][:, 0:n],
                op0=ALU.mult, op1=ALU.mult, accum_out=stat["ssum", s][:],
            )

        def log_table(s):
            nc.scalar.activation(stat["y", s][:, 0:1], stat["ssum", s][:], ACT.Ln, scale=1.0 / J)

        def log_offset(s):
            nc.scalar.activation(
                stat["nco", s][:], stat["y", s][:, 0:1], ACT.Identity, scale=-1.0, bias=stat["negm", s][:]
            )

        def guess(s):
            nc.scalar.activation(
                stat["y", s][:, 0:1], stat["ssum", s][:].bitcast(U32), ACT.Copy,
                scale=LN2 * 2.0**-23, bias=-(127.0 - 0.043 + 11.0) * LN2,
            )
            nc.scalar.activation(stat["sj", s][:], stat["ssum", s][:], ACT.Copy, scale=1.0 / J)

        def newton_exp(s, i):
            ee, y = stat["ee", s], stat["y", s]
            if i == 0:
                nc.scalar.activation(ee[:, 0:1], y[:, 0:1], ACT.Exp, scale=-1.0)
            else:
                nc.scalar.activation(ee[:, i : i + 1], y[:, i : i + 1], ACT.Exp, scale=-1.0, bias=consts[:, i - 1 : i])

        def newton_step(s, i):
            ee, y = stat["ee", s], stat["y", s]
            nc.scalar.activation(
                y[:, i + 1 : i + 2], ee[:, i : i + 1], ACT.Identity, scale=stat["sj", s][:], bias=y[:, i : i + 1]
            )

        def offset(s):
            nc.scalar.activation(stat["nmc", s][:], stat["negm", s][:], ACT.Identity, bias=consts[:, NEWTON - 1 : NEWTON])
            nc.scalar.activation(
                stat["nco", s][:], stat["y", s][:, NEWTON : NEWTON + 1], ACT.Identity,
                scale=-1.0, bias=stat["nmc", s][:],
            )

        def finish(s, i, n, eng):
            cols = slice(J // n * i, J // n * (i + 1))
            nco = stat["nco", s]
            if eng == "g":
                nc.gpsimd.tensor_scalar(l_sb[:, s, cols], l_sb[:, s, cols], 1.0, nco[:], op0=ALU.mult, op1=ALU.add)
            elif eng == "v":
                nc.vector.tensor_scalar(l_sb[:, s, cols], l_sb[:, s, cols], nco[:], None, op0=ALU.add)
            else:
                nc.scalar.activation(l_sb[:, s, cols], l_sb[:, s, cols], ACT.Identity, bias=nco[:])

        def finish_first(s, i, n):
            cols = slice(J // n * i, J // n * (i + 1))
            nc.vector.tensor_scalar(
                l_sb[:, s, cols], l_sb[:, s, cols], stat["y", s][:, 0:1], stat["negm", s][:],
                op0=ALU.subtract, op1=ALU.add,
            )

        def store(s, i, n):
            cols = slice(J // n * i, J // n * (i + 1))
            nc.sync.dma_start(out=out_v[:, s, cols], in_=l_sb[:, s, cols])

        def early(h):
            cols = slice(256 * h, 256 * h + 256)
            nc.vector.tensor_copy(out=pg[:, cols, 0:2], in_=l_sb[:, 0:2, cols].rearrange("p t m -> p m t"))

        def late(c, eng):
            cols = slice(512 * c, 512 * c + 512)
            src = l_sb[:, 2:4, cols].rearrange("p t m -> p m t")
            if eng == "s":
                nc.scalar.copy(out=pg[:, cols, 2:4], in_=src)
            else:
                nc.vector.tensor_copy(out=pg[:, cols, 2:4], in_=src)

        def quant_out(c):
            cols = slice(512 * c, 512 * c + 512)
            nc.vector.quantize_mx(
                out=pcodes[:, cols].bitcast(FP8X4), scales=pscales[:, cols],
                in_=pg[:, cols, :].rearrange("p m t -> p (m t)"),
            )

        def store_words(c):
            cols = slice(512 * c, 512 * c + 512)
            nc.sync.dma_start(
                out=words_v[:, 2048 * c : 2048 * c + 2048].bitcast(I32), in_=pcodes[:, cols].bitcast(I32)
            )

        def store_scales(q):
            nc.scalar.dma_start(
                out=out_2[0, 4 * q : 4 * q + 4, :].bitcast(I32), in_=pscales[32 * q : 32 * q + 4, :].bitcast(I32)
            )

        V.memset(zeros[:], 0.0)
        V.memset(rows_h[:], 0.0)
        V.memset(wes_w, 0)
        S.dma_start(out=rows_h[0:2, :], in_=b_enc.rearrange("(c n) -> c n", c=2))
        V.memset(rows_g[:], 0.0)
        V.memset(warm[:], 0.0)
        V.memset(wds[:].bitcast(I32), 0)
        V.memset(rows_d[:], 0.0)
        make_identity(nc, ident[:])
        G.memset(consts[:, 0:1], 1.0)
        G.memset(consts[:, 1:2], 2.0)
        G.memset(consts[:, 2:3], 3.0)
        G.memset(consts[:, 3:4], 4.0)
        S.activation(warm[:, 1:2], warm[:, 0:1], ACT.Exp)
        V.tensor_copy(out=ident_bf[:], in_=ident[:])
        nc.sync.dma_start(out=x_sb[:, 0, 0:1024], in_=x_v[:, 0, 0:1024])
        nc.sync.dma_start(out=x_sb[:, 0, 1024:2048], in_=x_v[:, 0, 1024:2048])
        load_wes(0)
        load_wes(1)
        load_wes(2)
        load_wes(3)
        load_w(1)
        nc.sync.dma_start(out=rows_g[0:1, :], in_=g.rearrange("(c n) -> c n", c=1))
        load_w(0)
        nc.sync.dma_start(out=x_sb[:, 1, :], in_=x_v[:, 1, :])
        nc.sync.dma_start(out=eps_sb[:, 0:2, :], in_=eps_v[:, 0:2, :])
        nc.sync.dma_start(out=rows_d[0:4, :], in_=b_dec.rearrange("(c n) -> c n", c=4))
        nc.sync.dma_start(out=x_sb[:, 2, :], in_=x_v[:, 2, :])
        load_wds(0)
        load_wds(1)
        load_wds(2)
        load_wds(3)
        nc.sync.dma_start(out=wd[:].bitcast(I32), in_=w_dec_words[0].bitcast(I32))
        nc.sync.dma_start(out=x_sb[:, 3, :], in_=x_v[:, 3, :])
        nc.sync.dma_start(out=eps_sb[:, 2:4, :], in_=eps_v[:, 2:4, :])
        warm_up(bx[0])
        warm_up(bx[1])
        warm_up(bx[0])
        warm_up(bx[1])
        warm_up(bx[0])
        turn_x(0, 0, bx[0])
        spread(rows_h, 1, bl[0])
        warm_up(bx[1])
        spread(rows_h, 0, bl[2])
        turn_x(0, 1, bx[1])
        move_x(0, 0, bx[0], "s")
        S.copy(out=bmu[:], in_=bl[2][:])
        S.copy(out=blv[:], in_=bl[0][:])
        quant_x(0, 0)
        move_x(0, 1, bx[1], "v")
        quant_x(0, 1)
        spread(rows_g, 0, bl[1])
        hidden(0, 1, bh[0], (0, 1))
        hidden(0, 1, bh[0], (2, 3))
        S.copy(out=gb[:], in_=bl[1][:])
        hidden(0, 0, bh[1], (0, 1))
        hidden(0, 0, bh[1], (2, 3))
        turn_x(1, 1, bx[1])
        turn_x(1, 0, bx[0])
        spread(rows_d, 0, bl[0])
        spread(rows_d, 1, bl[1])
        G.tensor_tensor(bmug[:], bmu[:], gb[:], op=ALU.mult)
        eps_gain(0, G)
        eps_gain(1, G)
        lv_bias(0, bh[0])
        mu_gain(0, bh[1])
        lv_exp(0)
        move_x(1, 1, bx[1], "s")
        move_x(1, 0, bx[0], "s")
        turn_x(2, 1, bx[1])
        turn_x(2, 0, bx[0])
        mu_bias(0, V)
        noise(0, V)
        quant_x(1)
        S.copy(out=bdec[:, 0:512], in_=bl[0][:])
        S.copy(out=bdec[:, 512:1024], in_=bl[1][:])
        move_x(2, 1, bx[1], "s")
        move_x(2, 0, bx[0], "s")
        latent(0, V)
        spread(rows_d, 2, bl[0])
        spread(rows_d, 3, bl[1])
        hidden(1, 1, bl[2], (0, 1))
        hidden(1, 1, bl[2], (2, 3))
        turn_z(0, bx[0])
        hidden(1, 0, bl[3], (0, 1))
        hidden(1, 0, bl[3], (2, 3))
        S.copy(out=bdec[:, 1024:1536], in_=bl[0][:])
        S.copy(out=bdec[:, 1536:2048], in_=bl[1][:])
        move_z(0, bx[0])
        lv_bias(1, bl[2])
        quant_x(2)
        quant_z(0)
        mu_gain(1, bl[3])
        lv_exp(1)
        noise(1, V)
        mu_bias(1, G)
        eps_gain(2, G)
        latent(1, G)
        turn_x(3, 0, bx[0])
        decode(0, 0)
        decode(0, 2)
        decode(0, 1)
        hidden(2, 0, bh[1], (0, 1))
        decode(0, 3)
        hidden(2, 0, bh[1], (2, 3))
        turn_x(3, 1, bx[1])
        hidden(2, 1, bh[0], (0, 1))
        hidden(2, 1, bh[0], (2, 3))
        move_x(3, 1, bx[1], "s")
        move_x(3, 0, bx[0], "s")
        warm_up(bx[1])
        turn_z(1, bx[0])
        add_bias(0, 0)
        add_bias(0, 1)
        add_bias(0, 2)
        part_max(0, 0, 2)
        add_bias(0, 3)
        mu_gain(2, bh[1])
        lv_bias(2, bh[0])
        part_max(0, 1, 2)
        move_z(1, bx[0])
        lv_exp(2)
        quant_z(1)
        quant_x(3)
        noise(2, V)
        shift(0, 2)
        warm_up(bx[1])
        decode(1, 2)
        decode(1, 0)
        decode(1, 3)
        decode(1, 1)
        mu_bias(2, G)
        latent(2, G)
        drain(1, 0)
        full_exp(0)
        add_away(1, 0)
        eps_gain(3, G)
        hidden(3, 0, bh[1], (0, 1))
        hidden(3, 1, bh[0], (0, 1))
        hidden(3, 1, bh[0], (2, 3))
        turn_z(2, bx[1])
        hidden(3, 0, bh[1], (2, 3))
        add_bias(1, 2)
        add_bias(1, 3)
        add_bias(1, 1)
        part_max(1, 1, 2)
        lv_bias(3, bh[0])
        move_z(2, bx[1])
        guess(0)
        lv_exp(3)
        newton_exp(0, 0)
        newton_step(0, 0)
        newton_exp(0, 1)
        newton_step(0, 1)
        mu_gain(3, bh[1])
        quant_z(2)
        decode(2, 0)
        decode(2, 1)
        decode(2, 3)
        decode(2, 2)
        part_max(1, 0, 2)
        shift(1, 2)
        noise(3, V)
        mu_bias(3, G)
        latent(3, G)
        add_bias(2, 0)
        add_bias(2, 1)
        add_bias(2, 3)
        add_bias(2, 2)
        part_max(2, 0, 2)
        turn_z(3, bx[0])
        newton_exp(0, 2)
        full_exp(1)
        newton_step(0, 2)
        guess(1)
        newton_exp(0, 3)
        newton_exp(1, 0)
        move_z(3, bx[0])
        newton_step(1, 0)
        newton_step(0, 3)
        newton_exp(1, 1)
        offset(0)
        newton_step(1, 1)
        finish(0, 0, 4, "g")
        finish(0, 1, 4, "g")
        finish(0, 2, 4, "g")
        finish(0, 3, 4, "g")
        store(0, 0, 1)
        quant_z(3)
        part_max(2, 1, 2)
        decode(3, 0)
        decode(3, 3)
        decode(3, 2)
        decode(3, 1)
        newton_exp(1, 2)
        part_exp(2, 0, 2)
        add_bias(3, 0)
        shift(2, 2)
        add_bias(3, 3)
        newton_step(1, 2)
        part_exp(2, 1, 2)
        newton_exp(1, 3)
        correct(2, 2)
        newton_step(1, 3)
        offset(1)
        finish(1, 1, 4, "g")
        finish(1, 0, 4, "g")
        finish(1, 3, 4, "g")
        finish(1, 2, 4, "g")
        store(1, 0, 1)
        part_max(3, 0, 4)
        merge(2, 2)
        add_bias(3, 1)
        part_max(3, 3, 4)
        part_max(3, 1, 4)
        add_bias(3, 2)
        guess(2)
        part_max(3, 2, 4)
        early(0)
        early(5)
        shift(3, 4)
        early(2)
        newton_exp(2, 0)
        newton_step(2, 0)
        newton_exp(2, 1)
        part_exp(3, 0, 4)
        newton_step(2, 1)
        newton_exp(2, 2)
        part_exp(3, 1, 4)
        newton_step(2, 2)
        newton_exp(2, 3)
        part_exp(3, 3, 4)
        newton_step(2, 3)
        offset(2)
        part_exp(3, 2, 4)
        correct(3, 4)
        finish(2, 1, 4, "v")
        finish(2, 0, 4, "v")
        finish(2, 3, 4, "v")
        early(4)
        merge(3, 4)
        finish(2, 2, 4, "v")
        early(6)
        early(7)
        log_table(3)
        log_offset(3)
        store(2, 0, 2)
        finish_first(3, 0, 4)
        early(3)
        late(0, "v")
        early(1)
        store(2, 1, 2)
        finish(3, 1, 4, "s")
        finish(3, 3, 4, "s")
        finish(3, 2, 4, "s")
        store(3, 0, 4)
        store(3, 1, 4)
        store(3, 3, 4)
        store(3, 2, 4)
        late(1, "v")
        quant_out(0)
        late(3, "s")
        late(2, "s")
        store_words(0)
        quant_out(1)
        quant_out(3)
        quant_out(2)
        store_words(1)
        store_words(3)
        store_words(2)
        store_scales(0)
        store_scales(1)
        store_scales(2)
        store_scales(3)
